import numpy as np
import ml_dtypes


def mxq(x, axis, fmt="e4m3"):
    dtype, down = {"e4m3": (ml_dtypes.float8_e4m3fn, 7), "e5m2": (ml_dtypes.float8_e5m2, 14)}[fmt]
    v = np.moveaxis(np.asarray(x, np.float32).astype(ml_dtypes.bfloat16).astype(np.float64), axis, -1)
    blocks = v.reshape(v.shape[:-1] + (-1, 32))
    amax = np.abs(blocks).max(-1, keepdims=True)
    byte = np.maximum(np.where(amax > 0, np.frexp(amax)[1] - 1 + 127, 0) - down, 1)
    scale = np.exp2(byte - 127.0)
    codes = (blocks / scale).astype(np.float32).astype(dtype).astype(np.float64)
    return np.moveaxis((codes * scale).reshape(v.shape), -1, axis)


WIDE = False


def mx_kscale(k):
    if not WIDE:
        return np.ones(k)
    levels = np.array([10, -10, 5, -5, 0])
    if k % 512:
        return np.exp2(np.random.permutation(np.resize(levels, k // 32))).repeat(32)
    a = np.empty((k // 512, 16))
    for p in range(k // 512):
        a[p, :8] = np.random.permutation(np.resize(levels, 8))
        for g in range(8):
            far = levels[np.abs(levels - a[p, g]) >= 10]
            a[p, g + 8] = far[np.random.randint(len(far))]
    return np.exp2(a.ravel()).repeat(32)


def f64(x):
    return np.asarray(x).astype(np.float64)


def striped(idx):
    return np.tile(idx.reshape(-1, 16).T, (8, 1)).astype(np.uint16)


def unstriped(offs):
    return offs[:16].T.reshape(-1).astype(np.int64)


def pack_weight(w):
    k, n = w.shape
    w = f64(np.asarray(w, np.float32).astype(ml_dtypes.bfloat16)).reshape(k // 32, 32, n)
    amax = np.abs(w).max(1)
    byte = np.clip(np.where(amax > 0, np.frexp(amax)[1] - 1 + 127 - 7, 1), 1, 254)
    scaled = (w * np.exp2(127.0 - byte)[:, None, :]).reshape(k, n).astype(np.float32)
    words = np.ascontiguousarray(scaled.reshape(k // 512, 128, 4, n).transpose(0, 1, 3, 2)).astype(ml_dtypes.float8_e4m3fn).view(np.uint8)
    return words, np.ascontiguousarray(byte.astype(np.uint8).reshape(k // 512, 16, n))


def unpack_weight(words, scales):
    g, p, n, _ = words.shape
    vals = np.ascontiguousarray(words).view(ml_dtypes.float8_e4m3fn).astype(np.float64) * np.repeat(np.exp2(scales.astype(np.float64) - 127.0), 8, axis=1)[..., None]
    return vals.transpose(0, 1, 3, 2).reshape(g * 512, n)


def relu(v):
    return np.maximum(v, 0.0)


K, T, E, C, N = 2048, 768, 2, 256, 512


def by_expert(wq, xq):
    return np.concatenate([wq[e].T @ xq[:, e * C:(e + 1) * C] for e in range(E)], axis=1)


def setup_inputs():
    n = np.random.standard_normal
    s = mx_kscale(K)[:, None]
    packed = [pack_weight(m) for m in n((E, K, N)) / np.sqrt(K) / s[None]]
    return {
        "xT": (n((K, T)) * s).astype(np.float32),
        "xr": n((N, T)).astype(np.float32),
        "w_words": np.stack([m[0] for m in packed]),
        "w_scales": np.stack([m[1] for m in packed]),
        "b": (0.3 * n((N, E))).astype(np.float32),
        "gate": np.tile(np.random.uniform(0.2, 1.0, E * C), (N, 1)).astype(np.float32),
        "offs": striped(np.random.permutation(T)[:E * C]),
    }


def reference(xT, xr, w_words, w_scales, b, gate, offs):
    idx = unstriped(offs)
    w = np.stack([unpack_weight(w_words[e], w_scales[e]) for e in range(E)])
    xq = mxq(f64(xT)[:, idx], 0, "e4m3")
    y = by_expert(w, xq)
    y = relu(y + np.repeat(f64(b), C, axis=1))
    out = f64(xr).copy()
    out[:, idx] += f64(gate) * y
    return out

@@ -1,0 +1,213 @@
+from contextlib import ExitStack
+
+import concourse.mybir as mybir
+from concourse.masks import make_identity
+
+K, T, E, C, N = 2048, 768, 2, 256, 512
+P = 128
+PACK = 4
+K_PASS = P * PACK
+PASSES = K // K_PASS
+N_TILES = N // P
+LIST = C // 16
+HALVES = C // P
+ROWS = 4
+
+F32 = mybir.dt.float32
+BF16 = mybir.dt.bfloat16
+I32 = mybir.dt.int32
+U32 = mybir.dt.uint32
+U16 = mybir.dt.uint16
+U8 = mybir.dt.uint8
+FP8X4 = mybir.dt.float8_e4m3fn_x4
+COPY = mybir.ActivationFunctionType.Copy
+RELU = mybir.ActivationFunctionType.Relu
+ADD = mybir.AluOpType.add
+MULT = mybir.AluOpType.mult
+
+FLOPS = 2 * K * N * E * C
+BYTES = 4 * K * T + 2 * 4 * N * T + E * K * N + E * (K // 32) * N + 4 * N * E + 4 * E * C + 2 * P * E * LIST
+
+LOADS = (
+    ((0, 768),),
+    ((0, 768),),
+    ((0, 384), (384, 768)),
+    ((0, 256), (256, 512), (512, 768)),
+)
+GROUPS = (
+    ((0, 256, "vector"), (256, 512, "vector"), (512, 768, "scalar")),
+    ((0, 256, "scalar"), (256, 768, "vector")),
+    ((0, 512, "scalar"), (512, 768, "vector")),
+    ((0, 256, "scalar"), (256, 512, "scalar"), (512, 768, "vector")),
+)
+COPIED_UNITS = ((1, 1), (1, 2), (0, 3), (1, 3))
+
+
+def tile_moe_res_lin_relu_kernel(tc, xT, xr, w_words, w_scales, b, gate, offs, out):
+    nc = tc.nc
+
+    with ExitStack() as ctx:
+        keep = ctx.enter_context(tc.tile_pool(name="keep", bufs=1))
+        psum = ctx.enter_context(tc.psum_pool(name="psum", bufs=1))
+
+        def slots(e):
+            return slice(e * C, (e + 1) * C)
+
+        def places(e):
+            return slice(e * LIST, (e + 1) * LIST)
+
+        token_plane = keep.tile([P, T], U8, name="token_plane", align_bytes=64)
+        nc.gpsimd.memset(token_plane[:], 0)
+        weight_planes = []
+        for e in range(E):
+            plane = keep.tile([P, N], U8, name=f"weight_plane{e}", align_bytes=64)
+            nc.vector.memset(plane[:].bitcast(I32), 0)
+            for quadrant in range(4):
+                nc.gpsimd.dma_start(
+                    out=plane[32 * quadrant : 32 * quadrant + ROWS * PASSES, :].bitcast(I32),
+                    in_=w_scales[e, :, ROWS * quadrant : ROWS * (quadrant + 1), :].bitcast(I32),
+                )
+            weight_planes.append(plane)
+
+        windows = []
+        for n in range(N_TILES):
+            window = keep.tile([P, T], F32, name=f"window{n}")
+            nc.vector.memset(window[:], 0.0)
+            windows.append(window)
+
+        identity = keep.tile([P, P], F32, name="identity")
+        make_identity(nc, identity[:])
+
+        bias = keep.tile([P, N_TILES, E], F32, name="bias")
+        nc.scalar.dma_start(out=bias[:], in_=b.rearrange("(n p) e -> p n e", p=P))
+
+        offsets = keep.tile([P, E * LIST], U16, name="offsets")
+        raw = {}
+        for a in range(PASSES):
+            rows = xT[a * K_PASS : (a + 1) * K_PASS, :].rearrange("(p j) t -> p j t", j=PACK)
+            for lo, hi in LOADS[a]:
+                raw[a, lo] = keep.tile([P, PACK, hi - lo], F32, name=f"raw{a}_{lo}")
+                nc.sync.dma_start(out=raw[a, lo][:], in_=rows[:, :, lo:hi])
+            if a == 0:
+                nc.sync.dma_start(offsets[:], offs)
+
+        weights = [keep.tile([P, PASSES, N * PACK], U8, name=f"weights{e}", align_bytes=64) for e in range(E)]
+
+        def load_weights(e):
+            words = w_words[e].rearrange("a p n r -> p a (n r)")
+            nc.sync.dma_start(out=weights[e][:].bitcast(I32), in_=words.bitcast(I32))
+
+        load_weights(0)
+        gates = keep.tile([P, E * C], F32, name="gates")
+        nc.sync.dma_start(out=gates[:], in_=gate[0:P, :])
+        load_weights(1)
+        residuals = []
+        for n in range(N_TILES):
+            residual = keep.tile([P, T], F32, name=f"residual{n}")
+            nc.sync.dma_start(out=residual[:], in_=xr[n * P : (n + 1) * P, :])
+            residuals.append(residual)
+
+        token_words = []
+        slot_words = []
+
+        def gather_words(a, columns, lists):
+            nc.vector.tensor_copy(slot_words[a][:, columns], token_words[a][:].indirect(offsets[:, lists]))
+
+        for a in range(PASSES):
+            words = keep.tile([P, T], U32, name=f"token_words{a}", align_bytes=64)
+            token_words.append(words)
+            slot_words.append(keep.tile([P, E * C], U32, name=f"slot_words{a}", align_bytes=64))
+            for lo, hi, engine in GROUPS[a]:
+                grouped = keep.tile([P, hi - lo, PACK], BF16, name=f"grouped{a}_{lo}", align_bytes=64)
+                copy = nc.scalar.copy if engine == "scalar" else nc.vector.tensor_copy
+                for start, end in LOADS[a]:
+                    first, last = max(lo, start), min(hi, end)
+                    if first < last:
+                        copy(
+                            out=grouped[:, first - lo : last - lo, :].rearrange("p (c i) j -> p c j i", i=4),
+                            in_=raw[a, start][:, :, first - start : last - start].rearrange("p j (c i) -> p c j i", i=4),
+                        )
+                nc.vector.quantize_mx(
+                    out=words[:, lo:hi].bitcast(FP8X4),
+                    scales=token_plane[ROWS * a : P, lo:hi],
+                    in_=grouped[:].rearrange("p t j -> p (t j)"),
+                )
+            if a < PASSES - 2:
+                gather_words(a, slice(0, E * C), slice(0, E * LIST))
+
+        slot_plane = keep.tile([P, E * C], U8, name="slot_plane", align_bytes=64)
+        for e in range(E):
+            gather_words(PASSES - 2, slots(e), places(e))
+            gather_words(PASSES - 1, slots(e), places(e))
+            nc.vector.tensor_copy(slot_plane[:, slots(e)], token_plane[:].indirect(offsets[:, places(e)]))
+
+        relu = {}
+
+        def expert_unit(e, n, bank):
+            acc = psum.tile([P, C], F32, name=f"acc{e}_{n}", tag=f"bank{bank}")
+            for a in range(PASSES):
+                nc.tensor.matmul_mx(
+                    out=acc[:],
+                    lhsT=weights[e][:, a, n * P * PACK : (n + 1) * P * PACK].bitcast(FP8X4),
+                    lhsT_scale=weight_planes[e][ROWS * a : P, n * P : (n + 1) * P],
+                    rhs=slot_words[a][:, slots(e)].bitcast(FP8X4),
+                    rhs_scale=slot_plane[ROWS * a : P, slots(e)],
+                    start=(a == 0),
+                    stop=(a == PASSES - 1),
+                )
+            relu[e, n] = keep.tile([P, C], F32, name=f"relu{e}_{n}")
+            nc.scalar.activation(out=relu[e, n][:], in_=acc[:], func=RELU, bias=bias[:, n, e : e + 1])
+
+        def scatter_product(e, n):
+            nc.vector.tensor_tensor(windows[n][:].indirect(offsets[:, places(e)]), relu[e, n][:], gates[:, slots(e)], MULT)
+
+        def finish(n, lo, hi, engine, queue):
+            result = keep.tile([P, hi - lo], F32, name=f"result{n}_{lo}")
+            engine.tensor_tensor(result[:], windows[n][:, lo:hi], residuals[n][:, lo:hi], ADD)
+            queue.dma_start(out=out[n * P : (n + 1) * P, lo:hi], in_=result[:])
+
+        for n in range(N_TILES):
+            expert_unit(0, n, n)
+            if n < N_TILES - 1:
+                scatter_product(0, n)
+
+        gate_bank = psum.tile([P, E * HALVES, P], F32, name="gate_bank", tag="bank0")
+        for i in range(E * HALVES):
+            nc.tensor.transpose(gate_bank[:, i, :], gates[:, i * P : (i + 1) * P], identity[:])
+        gate_columns = keep.tile([P, E * HALVES], F32, name="gate_columns")
+        nc.scalar.copy(out=gate_columns[:], in_=gate_bank[:, :, 0])
+
+        for n in (1, 2, 3, 0):
+            expert_unit(1, n, N_TILES + (n + 3) % N_TILES)
+        scatter_product(1, 0)
+
+        products = {}
+
+        def gate_product(e, tiles, turned_banks, back_banks):
+            turned = keep.tile([P, HALVES, len(tiles), P], F32, name=f"turned{e}_{tiles[0]}")
+            for h in range(HALVES):
+                bank = psum.tile([P, len(tiles), P], F32, name=f"turned_bank{e}_{tiles[0]}_{h}", tag=f"bank{turned_banks[h]}")
+                for i, n in enumerate(tiles):
+                    nc.tensor.transpose(bank[:, i, :], relu[e, n][:, h * P : (h + 1) * P], identity[:])
+                column = e * HALVES + h
+                nc.scalar.activation(
+                    out=turned[:, h, :, :], in_=bank[:], func=COPY, scale=gate_columns[:, column : column + 1]
+                )
+            for i, n in enumerate(tiles):
+                bank = psum.tile([P, C], F32, name=f"back_bank{e}_{n}", tag=f"bank{back_banks[i]}")
+                for h in range(HALVES):
+                    nc.tensor.transpose(bank[:, h * P : (h + 1) * P], turned[:, h, i, :], identity[:])
+                products[e, n] = keep.tile([P, C], F32, name=f"product{e}_{n}")
+                nc.scalar.copy(out=products[e, n][:], in_=bank[:])
+
+        gate_product(1, (1,), (1, 2), (3,))
+        gate_product(1, (2, 3), (0, 4), (5, 6))
+        gate_product(0, (3,), (1, 2), (3,))
+
+        finish(0, 0, T, nc.gpsimd, nc.sync)
+        for e, n in COPIED_UNITS:
+            nc.vector.tensor_copy(windows[n][:].indirect(offsets[:, places(e)]), products[e, n][:])
+            if n < N_TILES - 1:
+                finish(n, 0, T, nc.gpsimd, nc.sync)
+        finish(N_TILES - 1, 0, T // 2, nc.vector, nc.scalar)
+        finish(N_TILES - 1, T // 2, T, nc.vector, nc.sync)

@@ -28,19 +28,11 @@ MULT = mybir.AluOpType.mult
 FLOPS = 2 * K * N * E * C
 BYTES = 4 * K * T + 2 * 4 * N * T + E * K * N + E * (K // 32) * N + 4 * N * E + 4 * E * C + 2 * P * E * LIST
 
-LOADS = (
-    ((0, 768),),
-    ((0, 768),),
-    ((0, 384), (384, 768)),
-    ((0, 256), (256, 512), (512, 768)),
-)
-GROUPS = (
-    ((0, 256, "vector"), (256, 512, "vector"), (512, 768, "scalar")),
-    ((0, 256, "scalar"), (256, 768, "vector")),
-    ((0, 512, "scalar"), (512, 768, "vector")),
-    ((0, 256, "scalar"), (256, 512, "scalar"), (512, 768, "vector")),
-)
-COPIED_UNITS = ((1, 1), (1, 2), (0, 3), (1, 3))
+WHOLE = ((0, T),)
+LOADS = (WHOLE, WHOLE, WHOLE, ((0, 512), (512, T)))
+EARLY_GROUPS = ((0, 256, 256), (384, 384, 640), (640, 640, T), (256, 384, 384))
+LAST_GROUPS = ((0, 0, 256), (256, 512, 512), (512, 640, T))
+GROUPS = (EARLY_GROUPS, EARLY_GROUPS, EARLY_GROUPS, LAST_GROUPS)
 
 
 def tile_moe_res_lin_relu_kernel(tc, xT, xr, w_words, w_scales, b, gate, offs, out):
@@ -56,27 +48,22 @@ def tile_moe_res_lin_relu_kernel(tc, xT, xr, w_words, w_scales, b, gate, offs, o
         def places(e):
             return slice(e * LIST, (e + 1) * LIST)
 
-        token_plane = keep.tile([P, T], U8, name="token_plane", align_bytes=64)
-        nc.gpsimd.memset(token_plane[:], 0)
+        identity = keep.tile([P, P], F32, name="identity")
+        make_identity(nc, identity[:])
+
         weight_planes = []
         for e in range(E):
             plane = keep.tile([P, N], U8, name=f"weight_plane{e}", align_bytes=64)
             nc.vector.memset(plane[:].bitcast(I32), 0)
-            for quadrant in range(4):
-                nc.gpsimd.dma_start(
-                    out=plane[32 * quadrant : 32 * quadrant + ROWS * PASSES, :].bitcast(I32),
-                    in_=w_scales[e, :, ROWS * quadrant : ROWS * (quadrant + 1), :].bitcast(I32),
-                )
             weight_planes.append(plane)
+        token_plane = keep.tile([P, T], U8, name="token_plane", align_bytes=64)
+        nc.vector.memset(token_plane[:].bitcast(I32), 0)
 
         windows = []
         for n in range(N_TILES):
             window = keep.tile([P, T], F32, name=f"window{n}")
             nc.vector.memset(window[:], 0.0)
             windows.append(window)
-
-        identity = keep.tile([P, P], F32, name="identity")
-        make_identity(nc, identity[:])
 
         bias = keep.tile([P, N_TILES, E], F32, name="bias")
         nc.scalar.dma_start(out=bias[:], in_=b.rearrange("(n p) e -> p n e", p=P))
@@ -91,16 +78,29 @@ def tile_moe_res_lin_relu_kernel(tc, xT, xr, w_words, w_scales, b, gate, offs, o
             if a == 0:
                 nc.sync.dma_start(offsets[:], offs)
 
-        weights = [keep.tile([P, PASSES, N * PACK], U8, name=f"weights{e}", align_bytes=64) for e in range(E)]
+        weights = {}
 
-        def load_weights(e):
-            words = w_words[e].rearrange("a p n r -> p a (n r)")
-            nc.sync.dma_start(out=weights[e][:].bitcast(I32), in_=words.bitcast(I32))
+        def load_weights(e, tiles):
+            words = w_words[e].rearrange("a p n r -> p a (n r)")[:, :, tiles[0] * P * PACK : (tiles[-1] + 1) * P * PACK]
+            tile = keep.tile([P, PASSES, len(tiles) * P * PACK], U8, name=f"weights{e}_{tiles[0]}", align_bytes=64)
+            nc.sync.dma_start(out=tile[:].bitcast(I32), in_=words.bitcast(I32))
+            for i, n in enumerate(tiles):
+                weights[e, n] = tile, i
 
-        load_weights(0)
+        def load_scales(e):
+            for quadrant in range(4):
+                nc.sync.dma_start(
+                    out=weight_planes[e][32 * quadrant : 32 * quadrant + ROWS * PASSES, :].bitcast(I32),
+                    in_=w_scales[e, :, ROWS * quadrant : ROWS * (quadrant + 1), :].bitcast(I32),
+                )
+
+        load_scales(0)
+        load_weights(0, (0, 1))
+        load_weights(0, (2, 3))
         gates = keep.tile([P, E * C], F32, name="gates")
         nc.sync.dma_start(out=gates[:], in_=gate[0:P, :])
-        load_weights(1)
+        load_scales(1)
+        load_weights(1, (0, 1, 2, 3))
         residuals = []
         for n in range(N_TILES):
             residual = keep.tile([P, T], F32, name=f"residual{n}")
@@ -108,7 +108,15 @@ def tile_moe_res_lin_relu_kernel(tc, xT, xr, w_words, w_scales, b, gate, offs, o
             residuals.append(residual)
 
         token_words = []
-        slot_words = []
+        slot_words = {}
+
+        def interleave(a, grouped, lo, first, last, copy):
+            for start, end in LOADS[a]:
+                if start <= first < last <= end:
+                    copy(
+                        out=grouped[:, first - lo : last - lo, :].rearrange("p (c i) j -> p c j i", i=4),
+                        in_=raw[a, start][:, :, first - start : last - start].rearrange("p j (c i) -> p c j i", i=4),
+                    )
 
         def gather_words(a, columns, lists):
             nc.vector.tensor_copy(slot_words[a][:, columns], token_words[a][:].indirect(offsets[:, lists]))
@@ -116,24 +124,24 @@ def tile_moe_res_lin_relu_kernel(tc, xT, xr, w_words, w_scales, b, gate, offs, o
         for a in range(PASSES):
             words = keep.tile([P, T], U32, name=f"token_words{a}", align_bytes=64)
             token_words.append(words)
-            slot_words.append(keep.tile([P, E * C], U32, name=f"slot_words{a}", align_bytes=64))
-            for lo, hi, engine in GROUPS[a]:
-                grouped = keep.tile([P, hi - lo, PACK], BF16, name=f"grouped{a}_{lo}", align_bytes=64)
-                copy = nc.scalar.copy if engine == "scalar" else nc.vector.tensor_copy
-                for start, end in LOADS[a]:
-                    first, last = max(lo, start), min(hi, end)
-                    if first < last:
-                        copy(
-                            out=grouped[:, first - lo : last - lo, :].rearrange("p (c i) j -> p c j i", i=4),
-                            in_=raw[a, start][:, :, first - start : last - start].rearrange("p j (c i) -> p c j i", i=4),
-                        )
+            grouped = {}
+            for lo, mid, hi in GROUPS[a]:
+                grouped[lo] = keep.tile([P, hi - lo, PACK], BF16, name=f"grouped{a}_{lo}", tag=f"grouped{a}_{lo}", align_bytes=64)
+                interleave(a, grouped[lo], lo, lo, mid, nc.scalar.copy)
+                interleave(a, grouped[lo], lo, mid, hi, nc.vector.tensor_copy)
+            for lo, mid, hi in GROUPS[a]:
                 nc.vector.quantize_mx(
                     out=words[:, lo:hi].bitcast(FP8X4),
                     scales=token_plane[ROWS * a : P, lo:hi],
-                    in_=grouped[:].rearrange("p t j -> p (t j)"),
+                    in_=grouped[lo][:].rearrange("p t j -> p (t j)"),
                 )
             if a < PASSES - 2:
+                slot_words[a] = keep.tile([P, E * C], U32, name=f"slot_words{a}", align_bytes=64)
                 gather_words(a, slice(0, E * C), slice(0, E * LIST))
+
+        last_group = f"grouped{PASSES - 1}_{LAST_GROUPS[-1][0]}"
+        slot_words[PASSES - 2] = keep.tile([P, E * C], U32, name="slot_words2", tag=last_group, align_bytes=64)
+        slot_words[PASSES - 1] = keep.tile([P, E * C], U32, name="slot_words3", align_bytes=64)
 
         slot_plane = keep.tile([P, E * C], U8, name="slot_plane", align_bytes=64)
         for e in range(E):
@@ -145,10 +153,11 @@ def tile_moe_res_lin_relu_kernel(tc, xT, xr, w_words, w_scales, b, gate, offs, o
 
         def expert_unit(e, n, bank):
             acc = psum.tile([P, C], F32, name=f"acc{e}_{n}", tag=f"bank{bank}")
+            tile, i = weights[e, n]
             for a in range(PASSES):
                 nc.tensor.matmul_mx(
                     out=acc[:],
-                    lhsT=weights[e][:, a, n * P * PACK : (n + 1) * P * PACK].bitcast(FP8X4),
+                    lhsT=tile[:, a, i * P * PACK : (i + 1) * P * PACK].bitcast(FP8X4),
                     lhsT_scale=weight_planes[e][ROWS * a : P, n * P : (n + 1) * P],
                     rhs=slot_words[a][:, slots(e)].bitcast(FP8X4),
                     rhs_scale=slot_plane[ROWS * a : P, slots(e)],
@@ -177,10 +186,6 @@ def tile_moe_res_lin_relu_kernel(tc, xT, xr, w_words, w_scales, b, gate, offs, o
         gate_columns = keep.tile([P, E * HALVES], F32, name="gate_columns")
         nc.scalar.copy(out=gate_columns[:], in_=gate_bank[:, :, 0])
 
-        for n in (1, 2, 3, 0):
-            expert_unit(1, n, N_TILES + (n + 3) % N_TILES)
-        scatter_product(1, 0)
-
         products = {}
 
         def gate_product(e, tiles, turned_banks, back_banks):
@@ -200,12 +205,15 @@ def tile_moe_res_lin_relu_kernel(tc, xT, xr, w_words, w_scales, b, gate, offs, o
                 products[e, n] = keep.tile([P, C], F32, name=f"product{e}_{n}")
                 nc.scalar.copy(out=products[e, n][:], in_=bank[:])
 
-        gate_product(1, (1,), (1, 2), (3,))
-        gate_product(1, (2, 3), (0, 4), (5, 6))
-        gate_product(0, (3,), (1, 2), (3,))
+        for n in range(N_TILES):
+            expert_unit(1, n, N_TILES + n)
+        scatter_product(1, 0)
+        gate_product(1, (1,), (0, 1), (2,))
+        gate_product(1, (2, 3), (3, 4), (5, 0))
+        gate_product(0, (3,), (6, 7), (1,))
 
         finish(0, 0, T, nc.gpsimd, nc.sync)
-        for e, n in COPIED_UNITS:
+        for e, n in ((1, 1), (1, 2), (1, 3), (0, 3)):
             nc.vector.tensor_copy(windows[n][:].indirect(offsets[:, places(e)]), products[e, n][:])
             if n < N_TILES - 1:
                 finish(n, 0, T, nc.gpsimd, nc.sync)

@@ -30,7 +30,7 @@ BYTES = 4 * K * T + 2 * 4 * N * T + E * K * N + E * (K // 32) * N + 4 * N * E + 
 
 WHOLE = ((0, T),)
 LOADS = (WHOLE, WHOLE, WHOLE, ((0, 512), (512, T)))
-EARLY_GROUPS = ((0, 256, 256), (384, 384, 640), (640, 640, T), (256, 384, 384))
+EARLY_GROUPS = ((384, 384, 640), (0, 256, 256), (640, 640, T), (256, 384, 384))
 LAST_GROUPS = ((0, 0, 256), (256, 512, 512), (512, 640, T))
 GROUPS = (EARLY_GROUPS, EARLY_GROUPS, EARLY_GROUPS, LAST_GROUPS)
 
@@ -48,6 +48,10 @@ def tile_moe_res_lin_relu_kernel(tc, xT, xr, w_words, w_scales, b, gate, offs, o
         def places(e):
             return slice(e * LIST, (e + 1) * LIST)
 
+        short_rows = keep.tile([P, (E + 1) * P], F32, name="short_rows")
+        nc.gpsimd.memset(short_rows[:], 0.0)
+        nc.gpsimd.dma_start(out=short_rows[0:N_TILES, 0 : E * P], in_=b.rearrange("(n p) e -> n (p e)", p=P))
+        nc.gpsimd.dma_start(out=short_rows[0:N_TILES, E * P :], in_=gate[0, :].rearrange("(n p) -> n p", p=P))
         identity = keep.tile([P, P], F32, name="identity")
         make_identity(nc, identity[:])
 
@@ -65,15 +69,12 @@ def tile_moe_res_lin_relu_kernel(tc, xT, xr, w_words, w_scales, b, gate, offs, o
             nc.vector.memset(window[:], 0.0)
             windows.append(window)
 
-        bias = keep.tile([P, N_TILES, E], F32, name="bias")
-        nc.scalar.dma_start(out=bias[:], in_=b.rearrange("(n p) e -> p n e", p=P))
-
         offsets = keep.tile([P, E * LIST], U16, name="offsets")
         raw = {}
         for a in range(PASSES):
             rows = xT[a * K_PASS : (a + 1) * K_PASS, :].rearrange("(p j) t -> p j t", j=PACK)
             for lo, hi in LOADS[a]:
-                raw[a, lo] = keep.tile([P, PACK, hi - lo], F32, name=f"raw{a}_{lo}")
+                raw[a, lo] = keep.tile([P, PACK, hi - lo], F32, name=f"raw{a}_{lo}", tag=f"raw{a}_{lo}")
                 nc.sync.dma_start(out=raw[a, lo][:], in_=rows[:, :, lo:hi])
             if a == 0:
                 nc.sync.dma_start(offsets[:], offs)
@@ -97,10 +98,9 @@ def tile_moe_res_lin_relu_kernel(tc, xT, xr, w_words, w_scales, b, gate, offs, o
         load_scales(0)
         load_weights(0, (0, 1))
         load_weights(0, (2, 3))
-        gates = keep.tile([P, E * C], F32, name="gates")
-        nc.sync.dma_start(out=gates[:], in_=gate[0:P, :])
         load_scales(1)
-        load_weights(1, (0, 1, 2, 3))
+        load_weights(1, (0, 1))
+        load_weights(1, (2, 3))
         residuals = []
         for n in range(N_TILES):
             residual = keep.tile([P, T], F32, name=f"residual{n}")
@@ -149,6 +149,20 @@ def tile_moe_res_lin_relu_kernel(tc, xT, xr, w_words, w_scales, b, gate, offs, o
             gather_words(PASSES - 1, slots(e), places(e))
             nc.vector.tensor_copy(slot_plane[:, slots(e)], token_plane[:].indirect(offsets[:, places(e)]))
 
+        column_bank = psum.tile([P, E + 1, P], F32, name="column_bank", tag="bank0")
+        for e in range(E):
+            nc.tensor.transpose(column_bank[:, e, :], short_rows[:, e : E * P : E], identity[:])
+        nc.tensor.transpose(column_bank[:, E, :], short_rows[:, E * P :], identity[:])
+        columns = keep.tile([P, E + 1, N_TILES], F32, name="columns", tag=f"raw{PASSES - 1}_{LOADS[-1][-1][0]}")
+        nc.scalar.copy(out=columns[:], in_=column_bank[:, :, 0:N_TILES])
+        gate_columns = columns[:, E, :]
+
+        gate_bank = psum.tile([P, E * C], F32, name="gate_bank", tag="bank1")
+        for i in range(E * HALVES):
+            nc.tensor.transpose(gate_bank[:, i * P : (i + 1) * P], gate_columns[:, i : i + 1].to_broadcast([P, P]), identity[:])
+        gates = keep.tile([P, E * C], F32, name="gates")
+        nc.scalar.copy(out=gates[:], in_=gate_bank[:])
+
         relu = {}
 
         def expert_unit(e, n, bank):
@@ -165,7 +179,7 @@ def tile_moe_res_lin_relu_kernel(tc, xT, xr, w_words, w_scales, b, gate, offs, o
                     stop=(a == PASSES - 1),
                 )
             relu[e, n] = keep.tile([P, C], F32, name=f"relu{e}_{n}")
-            nc.scalar.activation(out=relu[e, n][:], in_=acc[:], func=RELU, bias=bias[:, n, e : e + 1])
+            nc.scalar.activation(out=relu[e, n][:], in_=acc[:], func=RELU, bias=columns[:, e, n : n + 1])
 
         def scatter_product(e, n):
             nc.vector.tensor_tensor(windows[n][:].indirect(offsets[:, places(e)]), relu[e, n][:], gates[:, slots(e)], MULT)
@@ -180,13 +194,7 @@ def tile_moe_res_lin_relu_kernel(tc, xT, xr, w_words, w_scales, b, gate, offs, o
             if n < N_TILES - 1:
                 scatter_product(0, n)
 
-        gate_bank = psum.tile([P, E * HALVES, P], F32, name="gate_bank", tag="bank0")
-        for i in range(E * HALVES):
-            nc.tensor.transpose(gate_bank[:, i, :], gates[:, i * P : (i + 1) * P], identity[:])
-        gate_columns = keep.tile([P, E * HALVES], F32, name="gate_columns")
-        nc.scalar.copy(out=gate_columns[:], in_=gate_bank[:, :, 0])
-
-        products = {}
+        products = {n: keep.tile([P, E * C], F32, name=f"products{n}") for n in range(1, N_TILES)}
 
         def gate_product(e, tiles, turned_banks, back_banks):
             turned = keep.tile([P, HALVES, len(tiles), P], F32, name=f"turned{e}_{tiles[0]}")
@@ -202,8 +210,7 @@ def tile_moe_res_lin_relu_kernel(tc, xT, xr, w_words, w_scales, b, gate, offs, o
                 bank = psum.tile([P, C], F32, name=f"back_bank{e}_{n}", tag=f"bank{back_banks[i]}")
                 for h in range(HALVES):
                     nc.tensor.transpose(bank[:, h * P : (h + 1) * P], turned[:, h, i, :], identity[:])
-                products[e, n] = keep.tile([P, C], F32, name=f"product{e}_{n}")
-                nc.scalar.copy(out=products[e, n][:], in_=bank[:])
+                nc.scalar.copy(out=products[n][:, slots(e)], in_=bank[:])
 
         for n in range(N_TILES):
             expert_unit(1, n, N_TILES + n)
@@ -213,9 +220,10 @@ def tile_moe_res_lin_relu_kernel(tc, xT, xr, w_words, w_scales, b, gate, offs, o
         gate_product(0, (3,), (6, 7), (1,))
 
         finish(0, 0, T, nc.gpsimd, nc.sync)
-        for e, n in ((1, 1), (1, 2), (1, 3), (0, 3)):
-            nc.vector.tensor_copy(windows[n][:].indirect(offsets[:, places(e)]), products[e, n][:])
-            if n < N_TILES - 1:
-                finish(n, 0, T, nc.gpsimd, nc.sync)
-        finish(N_TILES - 1, 0, T // 2, nc.vector, nc.scalar)
-        finish(N_TILES - 1, T // 2, T, nc.vector, nc.sync)
+        for n in range(1, N_TILES - 1):
+            nc.vector.tensor_copy(windows[n][:].indirect(offsets[:, places(1)]), products[n][:, slots(1)])
+            finish(n, 0, T, nc.gpsimd, nc.sync)
+        last = N_TILES - 1
+        nc.vector.tensor_copy(windows[last][:].indirect(offsets[:]), products[last][:])
+        for lo, queue in ((0, nc.sync), (256, nc.scalar), (512, nc.sync)):
+            finish(last, lo, lo + 256, nc.vector, queue)

@@ -30,7 +30,7 @@ BYTES = 4 * K * T + 2 * 4 * N * T + E * K * N + E * (K // 32) * N + 4 * N * E + 
 
 WHOLE = ((0, T),)
 LOADS = (WHOLE, WHOLE, WHOLE, ((0, 512), (512, T)))
-EARLY_GROUPS = ((384, 384, 640), (0, 256, 256), (640, 640, T), (256, 384, 384))
+EARLY_GROUPS = ((0, 0, 256), (256, 512, 512), (512, T, T))
 LAST_GROUPS = ((0, 0, 256), (256, 512, 512), (512, 640, T))
 GROUPS = (EARLY_GROUPS, EARLY_GROUPS, EARLY_GROUPS, LAST_GROUPS)
 
@@ -146,8 +146,8 @@ def tile_moe_res_lin_relu_kernel(tc, xT, xr, w_words, w_scales, b, gate, offs, o
         slot_plane = keep.tile([P, E * C], U8, name="slot_plane", align_bytes=64)
         for e in range(E):
             gather_words(PASSES - 2, slots(e), places(e))
-            gather_words(PASSES - 1, slots(e), places(e))
             nc.vector.tensor_copy(slot_plane[:, slots(e)], token_plane[:].indirect(offsets[:, places(e)]))
+            gather_words(PASSES - 1, slots(e), places(e))
 
         column_bank = psum.tile([P, E + 1, P], F32, name="column_bank", tag="bank0")
         for e in range(E):

@@ -30,9 +30,8 @@ BYTES = 4 * K * T + 2 * 4 * N * T + E * K * N + E * (K // 32) * N + 4 * N * E + 
 
 WHOLE = ((0, T),)
 LOADS = (WHOLE, WHOLE, WHOLE, ((0, 512), (512, T)))
-EARLY_GROUPS = ((0, 0, 256), (256, 512, 512), (512, T, T))
+EARLY_GROUPS = ((0, 128, 128), (128, 320, 640), (640, T, T))
 LAST_GROUPS = ((0, 0, 256), (256, 512, 512), (512, 640, T))
-GROUPS = (EARLY_GROUPS, EARLY_GROUPS, EARLY_GROUPS, LAST_GROUPS)
 
 
 def tile_moe_res_lin_relu_kernel(tc, xT, xr, w_words, w_scales, b, gate, offs, out):
@@ -121,23 +120,40 @@ def tile_moe_res_lin_relu_kernel(tc, xT, xr, w_words, w_scales, b, gate, offs, o
         def gather_words(a, columns, lists):
             nc.vector.tensor_copy(slot_words[a][:, columns], token_words[a][:].indirect(offsets[:, lists]))
 
+        grouped = {}
+
+        def interleave_group(a, lo, mid, hi):
+            tile = keep.tile([P, hi - lo, PACK], BF16, name=f"grouped{a}_{lo}", tag=f"grouped{a}_{lo}", align_bytes=64)
+            interleave(a, tile, lo, lo, mid, nc.scalar.copy)
+            interleave(a, tile, lo, mid, hi, nc.vector.tensor_copy)
+            grouped[a, lo] = tile
+
+        def quantise_group(a, lo, mid, hi):
+            nc.vector.quantize_mx(
+                out=token_words[a][:, lo:hi].bitcast(FP8X4),
+                scales=token_plane[ROWS * a : P, lo:hi],
+                in_=grouped[a, lo][:].rearrange("p t j -> p (t j)"),
+            )
+
         for a in range(PASSES):
-            words = keep.tile([P, T], U32, name=f"token_words{a}", align_bytes=64)
-            token_words.append(words)
-            grouped = {}
-            for lo, mid, hi in GROUPS[a]:
-                grouped[lo] = keep.tile([P, hi - lo, PACK], BF16, name=f"grouped{a}_{lo}", tag=f"grouped{a}_{lo}", align_bytes=64)
-                interleave(a, grouped[lo], lo, lo, mid, nc.scalar.copy)
-                interleave(a, grouped[lo], lo, mid, hi, nc.vector.tensor_copy)
-            for lo, mid, hi in GROUPS[a]:
-                nc.vector.quantize_mx(
-                    out=words[:, lo:hi].bitcast(FP8X4),
-                    scales=token_plane[ROWS * a : P, lo:hi],
-                    in_=grouped[lo][:].rearrange("p t j -> p (t j)"),
-                )
+            token_words.append(keep.tile([P, T], U32, name=f"token_words{a}", align_bytes=64))
+        for a in range(PASSES - 1):
+            for group in EARLY_GROUPS:
+                interleave_group(a, *group)
+            for group in EARLY_GROUPS[:-1]:
+                quantise_group(a, *group)
             if a < PASSES - 2:
+                quantise_group(a, *EARLY_GROUPS[-1])
                 slot_words[a] = keep.tile([P, E * C], U32, name=f"slot_words{a}", align_bytes=64)
                 gather_words(a, slice(0, E * C), slice(0, E * LIST))
+        own, other, shared = LAST_GROUPS
+        interleave_group(PASSES - 1, *own)
+        interleave_group(PASSES - 1, *other)
+        quantise_group(PASSES - 2, *EARLY_GROUPS[-1])
+        quantise_group(PASSES - 1, *own)
+        interleave_group(PASSES - 1, *shared)
+        quantise_group(PASSES - 1, *other)
+        quantise_group(PASSES - 1, *shared)
 
         last_group = f"grouped{PASSES - 1}_{LAST_GROUPS[-1][0]}"
         slot_words[PASSES - 2] = keep.tile([P, E * C], U32, name="slot_words2", tag=last_group, align_bytes=64)

@@ -31,7 +31,7 @@ BYTES = 4 * K * T + 2 * 4 * N * T + E * K * N + E * (K // 32) * N + 4 * N * E + 
 WHOLE = ((0, T),)
 LOADS = (WHOLE, WHOLE, WHOLE, ((0, 512), (512, T)))
 EARLY_GROUPS = ((0, 128, 128), (128, 320, 640), (640, T, T))
-LAST_GROUPS = ((0, 0, 256), (256, 512, 512), (512, 640, T))
+LAST_GROUPS = ((0, 0, 256), (256, 512, 512), (512, 576, T))
 
 
 def tile_moe_res_lin_relu_kernel(tc, xT, xr, w_words, w_scales, b, gate, offs, out):
@@ -155,7 +155,7 @@ def tile_moe_res_lin_relu_kernel(tc, xT, xr, w_words, w_scales, b, gate, offs, o
         quantise_group(PASSES - 1, *other)
         quantise_group(PASSES - 1, *shared)
 
-        last_group = f"grouped{PASSES - 1}_{LAST_GROUPS[-1][0]}"
+        last_group = f"grouped{PASSES - 1}_{other[0]}"
         slot_words[PASSES - 2] = keep.tile([P, E * C], U32, name="slot_words2", tag=last_group, align_bytes=64)
         slot_words[PASSES - 1] = keep.tile([P, E * C], U32, name="slot_words3", align_bytes=64)
 
@@ -238,8 +238,11 @@ def tile_moe_res_lin_relu_kernel(tc, xT, xr, w_words, w_scales, b, gate, offs, o
         finish(0, 0, T, nc.gpsimd, nc.sync)
         for n in range(1, N_TILES - 1):
             nc.vector.tensor_copy(windows[n][:].indirect(offsets[:, places(1)]), products[n][:, slots(1)])
-            finish(n, 0, T, nc.gpsimd, nc.sync)
+            if n < N_TILES - 2:
+                finish(n, 0, T, nc.gpsimd, nc.sync)
+        for lo in (0, T // 2):
+            finish(N_TILES - 2, lo, lo + T // 2, nc.gpsimd, nc.sync)
         last = N_TILES - 1
         nc.vector.tensor_copy(windows[last][:].indirect(offsets[:]), products[last][:])
-        for lo, queue in ((0, nc.sync), (256, nc.scalar), (512, nc.sync)):
-            finish(last, lo, lo + 256, nc.vector, queue)
+        for lo, queue in ((0, nc.scalar), (T // 2, nc.sync)):
+            finish(last, lo, lo + T // 2, nc.vector, queue)

@@ -28,10 +28,8 @@ MULT = mybir.AluOpType.mult
 FLOPS = 2 * K * N * E * C
 BYTES = 4 * K * T + 2 * 4 * N * T + E * K * N + E * (K // 32) * N + 4 * N * E + 4 * E * C + 2 * P * E * LIST
 
-WHOLE = ((0, T),)
-LOADS = (WHOLE, WHOLE, WHOLE, ((0, 512), (512, T)))
-EARLY_GROUPS = ((0, 128, 128), (128, 320, 640), (640, T, T))
-LAST_GROUPS = ((0, 0, 256), (256, 512, 512), (512, 576, T))
+GROUPS = ((0, 128, 128), (128, 256, 640), (640, T, T))
+FIRST = 128
 
 
 def tile_moe_res_lin_relu_kernel(tc, xT, xr, w_words, w_scales, b, gate, offs, out):
@@ -72,9 +70,8 @@ def tile_moe_res_lin_relu_kernel(tc, xT, xr, w_words, w_scales, b, gate, offs, o
         raw = {}
         for a in range(PASSES):
             rows = xT[a * K_PASS : (a + 1) * K_PASS, :].rearrange("(p j) t -> p j t", j=PACK)
-            for lo, hi in LOADS[a]:
-                raw[a, lo] = keep.tile([P, PACK, hi - lo], F32, name=f"raw{a}_{lo}", tag=f"raw{a}_{lo}")
-                nc.sync.dma_start(out=raw[a, lo][:], in_=rows[:, :, lo:hi])
+            raw[a] = keep.tile([P, PACK, T], F32, name=f"raw{a}", tag=f"raw{a}")
+            nc.sync.dma_start(out=raw[a][:], in_=rows)
             if a == 0:
                 nc.sync.dma_start(offsets[:], offs)
 
@@ -110,12 +107,11 @@ def tile_moe_res_lin_relu_kernel(tc, xT, xr, w_words, w_scales, b, gate, offs, o
         slot_words = {}
 
         def interleave(a, grouped, lo, first, last, copy):
-            for start, end in LOADS[a]:
-                if start <= first < last <= end:
-                    copy(
-                        out=grouped[:, first - lo : last - lo, :].rearrange("p (c i) j -> p c j i", i=4),
-                        in_=raw[a, start][:, :, first - start : last - start].rearrange("p j (c i) -> p c j i", i=4),
-                    )
+            if first < last:
+                copy(
+                    out=grouped[:, first - lo : last - lo, :].rearrange("p (c i) j -> p c j i", i=4),
+                    in_=raw[a][:, :, first:last].rearrange("p j (c i) -> p c j i", i=4),
+                )
 
         def gather_words(a, columns, lists):
             nc.vector.tensor_copy(slot_words[a][:, columns], token_words[a][:].indirect(offsets[:, lists]))
@@ -137,39 +133,28 @@ def tile_moe_res_lin_relu_kernel(tc, xT, xr, w_words, w_scales, b, gate, offs, o
 
         for a in range(PASSES):
             token_words.append(keep.tile([P, T], U32, name=f"token_words{a}", align_bytes=64))
-        for a in range(PASSES - 1):
-            for group in EARLY_GROUPS:
-                interleave_group(a, *group)
-            for group in EARLY_GROUPS[:-1]:
-                quantise_group(a, *group)
-            if a < PASSES - 2:
-                quantise_group(a, *EARLY_GROUPS[-1])
-                slot_words[a] = keep.tile([P, E * C], U32, name=f"slot_words{a}", align_bytes=64)
-                gather_words(a, slice(0, E * C), slice(0, E * LIST))
-        own, other, shared = LAST_GROUPS
-        interleave_group(PASSES - 1, *own)
-        interleave_group(PASSES - 1, *other)
-        quantise_group(PASSES - 2, *EARLY_GROUPS[-1])
-        quantise_group(PASSES - 1, *own)
-        interleave_group(PASSES - 1, *shared)
-        quantise_group(PASSES - 1, *other)
-        quantise_group(PASSES - 1, *shared)
+        def lists(columns):
+            return offsets[:, columns.start // 16 : columns.stop // 16]
 
-        last_group = f"grouped{PASSES - 1}_{other[0]}"
-        slot_words[PASSES - 2] = keep.tile([P, E * C], U32, name="slot_words2", tag=last_group, align_bytes=64)
-        slot_words[PASSES - 1] = keep.tile([P, E * C], U32, name="slot_words3", align_bytes=64)
+        for a in range(PASSES):
+            for group in GROUPS:
+                interleave_group(a, *group)
+            for group in GROUPS:
+                quantise_group(a, *group)
+            slot_words[a] = keep.tile([P, E * C], U32, name=f"slot_words{a}", align_bytes=64)
+            if a < PASSES - 1:
+                gather_words(a, slice(0, E * C), slice(0, E * LIST))
 
         slot_plane = keep.tile([P, E * C], U8, name="slot_plane", align_bytes=64)
-        for e in range(E):
-            gather_words(PASSES - 2, slots(e), places(e))
-            nc.vector.tensor_copy(slot_plane[:, slots(e)], token_plane[:].indirect(offsets[:, places(e)]))
-            gather_words(PASSES - 1, slots(e), places(e))
+        for columns in (slice(0, FIRST), slice(FIRST, C), slots(1)):
+            nc.vector.tensor_copy(slot_plane[:, columns], token_plane[:].indirect(lists(columns)))
+            nc.vector.tensor_copy(slot_words[PASSES - 1][:, columns], token_words[PASSES - 1][:].indirect(lists(columns)))
 
         column_bank = psum.tile([P, E + 1, P], F32, name="column_bank", tag="bank0")
         for e in range(E):
             nc.tensor.transpose(column_bank[:, e, :], short_rows[:, e : E * P : E], identity[:])
         nc.tensor.transpose(column_bank[:, E, :], short_rows[:, E * P :], identity[:])
-        columns = keep.tile([P, E + 1, N_TILES], F32, name="columns", tag=f"raw{PASSES - 1}_{LOADS[-1][-1][0]}")
+        columns = keep.tile([P, E + 1, N_TILES], F32, name="columns", tag=f"raw{PASSES - 1}")
         nc.scalar.copy(out=columns[:], in_=column_bank[:, :, 0:N_TILES])
         gate_columns = columns[:, E, :]
 
@@ -181,34 +166,44 @@ def tile_moe_res_lin_relu_kernel(tc, xT, xr, w_words, w_scales, b, gate, offs, o
 
         relu = {}
 
-        def expert_unit(e, n, bank):
-            acc = psum.tile([P, C], F32, name=f"acc{e}_{n}", tag=f"bank{bank}")
+        def expert_unit(e, n, bank, columns_of_slots, target):
+            width = columns_of_slots.stop - columns_of_slots.start
+            acc = psum.tile([P, width], F32, name=f"acc{e}_{n}_{columns_of_slots.start}", tag=f"bank{bank}")
             tile, i = weights[e, n]
             for a in range(PASSES):
                 nc.tensor.matmul_mx(
                     out=acc[:],
                     lhsT=tile[:, a, i * P * PACK : (i + 1) * P * PACK].bitcast(FP8X4),
                     lhsT_scale=weight_planes[e][ROWS * a : P, n * P : (n + 1) * P],
-                    rhs=slot_words[a][:, slots(e)].bitcast(FP8X4),
-                    rhs_scale=slot_plane[ROWS * a : P, slots(e)],
+                    rhs=slot_words[a][:, columns_of_slots].bitcast(FP8X4),
+                    rhs_scale=slot_plane[ROWS * a : P, columns_of_slots],
                     start=(a == 0),
                     stop=(a == PASSES - 1),
                 )
-            relu[e, n] = keep.tile([P, C], F32, name=f"relu{e}_{n}")
-            nc.scalar.activation(out=relu[e, n][:], in_=acc[:], func=RELU, bias=columns[:, e, n : n + 1])
+            nc.scalar.activation(out=target, in_=acc[:], func=RELU, bias=columns[:, e, n : n + 1])
 
-        def scatter_product(e, n):
-            nc.vector.tensor_tensor(windows[n][:].indirect(offsets[:, places(e)]), relu[e, n][:], gates[:, slots(e)], MULT)
+        def whole_unit(e, n, bank):
+            relu[e, n] = keep.tile([P, C], F32, name=f"relu{e}_{n}")
+            expert_unit(e, n, bank, slots(e), relu[e, n][:])
+
+        def scatter_product(n, values, columns_of_slots):
+            nc.vector.tensor_tensor(windows[n][:].indirect(lists(columns_of_slots)), values, gates[:, columns_of_slots], MULT)
 
         def finish(n, lo, hi, engine, queue):
             result = keep.tile([P, hi - lo], F32, name=f"result{n}_{lo}")
             engine.tensor_tensor(result[:], windows[n][:, lo:hi], residuals[n][:, lo:hi], ADD)
             queue.dma_start(out=out[n * P : (n + 1) * P, lo:hi], in_=result[:])
 
-        for n in range(N_TILES):
-            expert_unit(0, n, n)
-            if n < N_TILES - 1:
-                scatter_product(0, n)
+        first_relu = keep.tile([P, FIRST], F32, name="first_relu")
+        rest_relu = keep.tile([P, E * C - FIRST], F32, name="rest_relu")
+        expert_unit(0, 0, 0, slice(0, FIRST), first_relu[:])
+        scatter_product(0, first_relu[:], slice(0, FIRST))
+        for n in range(1, N_TILES - 1):
+            whole_unit(0, n, n + 1)
+            scatter_product(n, relu[0, n][:], slots(0))
+        expert_unit(0, 0, 4, slice(FIRST, C), rest_relu[:, : C - FIRST])
+        expert_unit(1, 0, 5, slots(1), rest_relu[:, C - FIRST :])
+        scatter_product(0, rest_relu[:], slice(FIRST, E * C))
 
         products = {n: keep.tile([P, E * C], F32, name=f"products{n}") for n in range(1, N_TILES)}
 
@@ -228,12 +223,12 @@ def tile_moe_res_lin_relu_kernel(tc, xT, xr, w_words, w_scales, b, gate, offs, o
                     nc.tensor.transpose(bank[:, h * P : (h + 1) * P], turned[:, h, i, :], identity[:])
                 nc.scalar.copy(out=products[n][:, slots(e)], in_=bank[:])
 
-        for n in range(N_TILES):
-            expert_unit(1, n, N_TILES + n)
-        scatter_product(1, 0)
-        gate_product(1, (1,), (0, 1), (2,))
-        gate_product(1, (2, 3), (3, 4), (5, 0))
-        gate_product(0, (3,), (6, 7), (1,))
+        for n, bank in ((1, 6), (2, 7), (3, 1)):
+            whole_unit(1, n, bank)
+        whole_unit(0, N_TILES - 1, 0)
+        gate_product(1, (1,), (2, 3), (4,))
+        gate_product(1, (2, 3), (5, 6), (7, 2))
+        gate_product(0, (3,), (3, 1), (4,))
 
         finish(0, 0, T, nc.gpsimd, nc.sync)
         for n in range(1, N_TILES - 1):

@@ -29,6 +29,8 @@ FLOPS = 2 * K * N * E * C
 BYTES = 4 * K * T + 2 * 4 * N * T + E * K * N + E * (K // 32) * N + 4 * N * E + 4 * E * C + 2 * P * E * LIST
 
 GROUPS = ((0, 128, 128), (128, 256, 640), (640, T, T))
+CUT = 512
+LAST_GROUPS = ((0, 256, 256), (CUT, CUT, T), (256, CUT, CUT))
 FIRST = 128
 
 
@@ -70,8 +72,9 @@ def tile_moe_res_lin_relu_kernel(tc, xT, xr, w_words, w_scales, b, gate, offs, o
         raw = {}
         for a in range(PASSES):
             rows = xT[a * K_PASS : (a + 1) * K_PASS, :].rearrange("(p j) t -> p j t", j=PACK)
-            raw[a] = keep.tile([P, PACK, T], F32, name=f"raw{a}", tag=f"raw{a}")
-            nc.sync.dma_start(out=raw[a][:], in_=rows)
+            for lo, hi in ((0, T),) if a < PASSES - 1 else ((0, CUT), (CUT, T)):
+                raw[a, lo] = keep.tile([P, PACK, hi - lo], F32, name=f"raw{a}_{lo}", tag=f"raw{a}_{lo}")
+                nc.sync.dma_start(out=raw[a, lo][:], in_=rows[:, :, lo:hi])
             if a == 0:
                 nc.sync.dma_start(offsets[:], offs)
 
@@ -108,9 +111,10 @@ def tile_moe_res_lin_relu_kernel(tc, xT, xr, w_words, w_scales, b, gate, offs, o
 
         def interleave(a, grouped, lo, first, last, copy):
             if first < last:
+                start = CUT if a == PASSES - 1 and first >= CUT else 0
                 copy(
                     out=grouped[:, first - lo : last - lo, :].rearrange("p (c i) j -> p c j i", i=4),
-                    in_=raw[a][:, :, first:last].rearrange("p j (c i) -> p c j i", i=4),
+                    in_=raw[a, start][:, :, first - start : last - start].rearrange("p j (c i) -> p c j i", i=4),
                 )
 
         def gather_words(a, columns, lists):
@@ -137,9 +141,10 @@ def tile_moe_res_lin_relu_kernel(tc, xT, xr, w_words, w_scales, b, gate, offs, o
             return offsets[:, columns.start // 16 : columns.stop // 16]
 
         for a in range(PASSES):
-            for group in GROUPS:
+            groups = GROUPS if a < PASSES - 1 else LAST_GROUPS
+            for group in groups:
                 interleave_group(a, *group)
-            for group in GROUPS:
+            for group in groups:
                 quantise_group(a, *group)
             slot_words[a] = keep.tile([P, E * C], U32, name=f"slot_words{a}", align_bytes=64)
             if a < PASSES - 1:
@@ -154,7 +159,7 @@ def tile_moe_res_lin_relu_kernel(tc, xT, xr, w_words, w_scales, b, gate, offs, o
         for e in range(E):
             nc.tensor.transpose(column_bank[:, e, :], short_rows[:, e : E * P : E], identity[:])
         nc.tensor.transpose(column_bank[:, E, :], short_rows[:, E * P :], identity[:])
-        columns = keep.tile([P, E + 1, N_TILES], F32, name="columns", tag=f"raw{PASSES - 1}")
+        columns = keep.tile([P, E + 1, N_TILES], F32, name="columns", tag=f"raw{PASSES - 1}_0")
         nc.scalar.copy(out=columns[:], in_=column_bank[:, :, 0:N_TILES])
         gate_columns = columns[:, E, :]
 

@@ -28,9 +28,10 @@ MULT = mybir.AluOpType.mult
 FLOPS = 2 * K * N * E * C
 BYTES = 4 * K * T + 2 * 4 * N * T + E * K * N + E * (K // 32) * N + 4 * N * E + 4 * E * C + 2 * P * E * LIST
 
-GROUPS = ((0, 128, 128), (128, 256, 640), (640, T, T))
-CUT = 512
-LAST_GROUPS = ((0, 256, 256), (CUT, CUT, T), (256, CUT, CUT))
+WHOLE = ((0, T),)
+LOADS = (WHOLE, WHOLE, ((0, 512), (512, T)), ((0, 256), (256, 512), (512, T)))
+HALF_EACH = ((0, 128, 128), (128, 256, 640), (640, T, T))
+GROUPS = (HALF_EACH, HALF_EACH, ((0, 256, 256), (512, 512, T), (256, 512, 512)), ((0, 256, 256), (256, 512, 512), (512, 608, T)))
 FIRST = 128
 
 
@@ -49,8 +50,6 @@ def tile_moe_res_lin_relu_kernel(tc, xT, xr, w_words, w_scales, b, gate, offs, o
 
         short_rows = keep.tile([P, (E + 1) * P], F32, name="short_rows")
         nc.gpsimd.memset(short_rows[:], 0.0)
-        nc.gpsimd.dma_start(out=short_rows[0:N_TILES, 0 : E * P], in_=b.rearrange("(n p) e -> n (p e)", p=P))
-        nc.gpsimd.dma_start(out=short_rows[0:N_TILES, E * P :], in_=gate[0, :].rearrange("(n p) -> n p", p=P))
         identity = keep.tile([P, P], F32, name="identity")
         make_identity(nc, identity[:])
 
@@ -72,11 +71,13 @@ def tile_moe_res_lin_relu_kernel(tc, xT, xr, w_words, w_scales, b, gate, offs, o
         raw = {}
         for a in range(PASSES):
             rows = xT[a * K_PASS : (a + 1) * K_PASS, :].rearrange("(p j) t -> p j t", j=PACK)
-            for lo, hi in ((0, T),) if a < PASSES - 1 else ((0, CUT), (CUT, T)):
+            for lo, hi in LOADS[a]:
                 raw[a, lo] = keep.tile([P, PACK, hi - lo], F32, name=f"raw{a}_{lo}", tag=f"raw{a}_{lo}")
                 nc.sync.dma_start(out=raw[a, lo][:], in_=rows[:, :, lo:hi])
             if a == 0:
                 nc.sync.dma_start(offsets[:], offs)
+                nc.sync.dma_start(out=short_rows[0:N_TILES, 0 : E * P], in_=b.rearrange("(n p) e -> n (p e)", p=P))
+                nc.sync.dma_start(out=short_rows[0:N_TILES, E * P :], in_=gate[0, :].rearrange("(n p) -> n p", p=P))
 
         weights = {}
 
@@ -111,7 +112,7 @@ def tile_moe_res_lin_relu_kernel(tc, xT, xr, w_words, w_scales, b, gate, offs, o
 
         def interleave(a, grouped, lo, first, last, copy):
             if first < last:
-                start = CUT if a == PASSES - 1 and first >= CUT else 0
+                start = max(piece[0] for piece in LOADS[a] if piece[0] <= first)
                 copy(
                     out=grouped[:, first - lo : last - lo, :].rearrange("p (c i) j -> p c j i", i=4),
                     in_=raw[a, start][:, :, first - start : last - start].rearrange("p j (c i) -> p c j i", i=4),
@@ -141,7 +142,7 @@ def tile_moe_res_lin_relu_kernel(tc, xT, xr, w_words, w_scales, b, gate, offs, o
             return offsets[:, columns.start // 16 : columns.stop // 16]
 
         for a in range(PASSES):
-            groups = GROUPS if a < PASSES - 1 else LAST_GROUPS
+            groups = GROUPS[a]
             for group in groups:
                 interleave_group(a, *group)
             for group in groups:
@@ -159,14 +160,14 @@ def tile_moe_res_lin_relu_kernel(tc, xT, xr, w_words, w_scales, b, gate, offs, o
         for e in range(E):
             nc.tensor.transpose(column_bank[:, e, :], short_rows[:, e : E * P : E], identity[:])
         nc.tensor.transpose(column_bank[:, E, :], short_rows[:, E * P :], identity[:])
-        columns = keep.tile([P, E + 1, N_TILES], F32, name="columns", tag=f"raw{PASSES - 1}_0")
+        columns = keep.tile([P, E + 1, N_TILES], F32, name="columns", tag="raw0_0")
         nc.scalar.copy(out=columns[:], in_=column_bank[:, :, 0:N_TILES])
         gate_columns = columns[:, E, :]
 
         gate_bank = psum.tile([P, E * C], F32, name="gate_bank", tag="bank1")
         for i in range(E * HALVES):
             nc.tensor.transpose(gate_bank[:, i * P : (i + 1) * P], gate_columns[:, i : i + 1].to_broadcast([P, P]), identity[:])
-        gates = keep.tile([P, E * C], F32, name="gates")
+        gates = keep.tile([P, E * C], F32, name="gates", tag="raw1_0")
         nc.scalar.copy(out=gates[:], in_=gate_bank[:])
 
         relu = {}

@@ -29,9 +29,9 @@ FLOPS = 2 * K * N * E * C
 BYTES = 4 * K * T + 2 * 4 * N * T + E * K * N + E * (K // 32) * N + 4 * N * E + 4 * E * C + 2 * P * E * LIST
 
 WHOLE = ((0, T),)
-LOADS = (WHOLE, WHOLE, ((0, 512), (512, T)), ((0, 256), (256, 512), (512, T)))
+LOADS = (WHOLE, WHOLE, WHOLE, ((0, 256), (256, 512), (512, T)))
 HALF_EACH = ((0, 128, 128), (128, 256, 640), (640, T, T))
-GROUPS = (HALF_EACH, HALF_EACH, ((0, 256, 256), (512, 512, T), (256, 512, 512)), ((0, 256, 256), (256, 512, 512), (512, 608, T)))
+GROUPS = (HALF_EACH, HALF_EACH, HALF_EACH, ((0, 256, 256), (256, 512, 512), (512, 640, T)))
 FIRST = 128
 
 
@@ -245,5 +245,5 @@ def tile_moe_res_lin_relu_kernel(tc, xT, xr, w_words, w_scales, b, gate, offs, o
             finish(N_TILES - 2, lo, lo + T // 2, nc.gpsimd, nc.sync)
         last = N_TILES - 1
         nc.vector.tensor_copy(windows[last][:].indirect(offsets[:]), products[last][:])
-        for lo, queue in ((0, nc.scalar), (T // 2, nc.sync)):
-            finish(last, lo, lo + T // 2, nc.vector, queue)
+        for lo, queue in ((0, nc.sync), (T // 3, nc.scalar), (2 * T // 3, nc.sync)):
+            finish(last, lo, lo + T // 3, nc.vector, queue)

@@ -114,8 +114,8 @@ def tile_moe_res_lin_relu_kernel(tc, xT, xr, w_words, w_scales, b, gate, offs, o
             if first < last:
                 start = max(piece[0] for piece in LOADS[a] if piece[0] <= first)
                 copy(
-                    out=grouped[:, first - lo : last - lo, :].rearrange("p (c i) j -> p c j i", i=4),
-                    in_=raw[a, start][:, :, first - start : last - start].rearrange("p j (c i) -> p c j i", i=4),
+                    out=grouped[:, first - lo : last - lo, :].rearrange("p (c i) j -> p c j i", i=2),
+                    in_=raw[a, start][:, :, first - start : last - start].rearrange("p j (c i) -> p c j i", i=2),
                 )
 
         def gather_words(a, columns, lists):

@@ -24,6 +24,7 @@ COPY = mybir.ActivationFunctionType.Copy
 RELU = mybir.ActivationFunctionType.Relu
 ADD = mybir.AluOpType.add
 MULT = mybir.AluOpType.mult
+MAX = mybir.AluOpType.max
 
 FLOPS = 2 * K * N * E * C
 BYTES = 4 * K * T + 2 * 4 * N * T + E * K * N + E * (K // 32) * N + 4 * N * E + 4 * E * C + 2 * P * E * LIST
@@ -97,15 +98,14 @@ def tile_moe_res_lin_relu_kernel(tc, xT, xr, w_words, w_scales, b, gate, offs, o
 
         load_scales(0)
         load_weights(0, (0, 1))
-        load_weights(0, (2, 3))
         load_scales(1)
         load_weights(1, (0, 1))
+        load_weights(0, (2, 3))
         load_weights(1, (2, 3))
-        residuals = []
-        for n in range(N_TILES):
-            residual = keep.tile([P, T], F32, name=f"residual{n}")
-            nc.sync.dma_start(out=residual[:], in_=xr[n * P : (n + 1) * P, :])
-            residuals.append(residual)
+        residuals = {}
+        for n in (0, 1, 3, 2):
+            residuals[n] = keep.tile([P, T], F32, name=f"residual{n}")
+            nc.sync.dma_start(out=residuals[n][:], in_=xr[n * P : (n + 1) * P, :])
 
         token_words = []
         slot_words = {}
@@ -117,9 +117,6 @@ def tile_moe_res_lin_relu_kernel(tc, xT, xr, w_words, w_scales, b, gate, offs, o
                     out=grouped[:, first - lo : last - lo, :].rearrange("p (c i) j -> p c j i", i=2),
                     in_=raw[a, start][:, :, first - start : last - start].rearrange("p j (c i) -> p c j i", i=2),
                 )
-
-        def gather_words(a, columns, lists):
-            nc.vector.tensor_copy(slot_words[a][:, columns], token_words[a][:].indirect(offsets[:, lists]))
 
         grouped = {}
 
@@ -147,14 +144,11 @@ def tile_moe_res_lin_relu_kernel(tc, xT, xr, w_words, w_scales, b, gate, offs, o
                 interleave_group(a, *group)
             for group in groups:
                 quantise_group(a, *group)
-            slot_words[a] = keep.tile([P, E * C], U32, name=f"slot_words{a}", align_bytes=64)
             if a < PASSES - 1:
-                gather_words(a, slice(0, E * C), slice(0, E * LIST))
-
-        slot_plane = keep.tile([P, E * C], U8, name="slot_plane", align_bytes=64)
-        for columns in (slice(0, FIRST), slice(FIRST, C), slots(1)):
-            nc.vector.tensor_copy(slot_plane[:, columns], token_plane[:].indirect(lists(columns)))
-            nc.vector.tensor_copy(slot_words[PASSES - 1][:, columns], token_words[PASSES - 1][:].indirect(lists(columns)))
+                gathered = keep.tile([P, E * C], U32, name=f"slot_words{a}", align_bytes=64)
+                nc.vector.tensor_copy(gathered[:], token_words[a][:].indirect(offsets[:]))
+                for e in range(E):
+                    slot_words[a, e] = gathered[:, slots(e)]
 
         column_bank = psum.tile([P, E + 1, P], F32, name="column_bank", tag="bank0")
         for e in range(E):
@@ -167,83 +161,90 @@ def tile_moe_res_lin_relu_kernel(tc, xT, xr, w_words, w_scales, b, gate, offs, o
         gate_bank = psum.tile([P, E * C], F32, name="gate_bank", tag="bank1")
         for i in range(E * HALVES):
             nc.tensor.transpose(gate_bank[:, i * P : (i + 1) * P], gate_columns[:, i : i + 1].to_broadcast([P, P]), identity[:])
-        gates = keep.tile([P, E * C], F32, name="gates", tag="raw1_0")
-        nc.scalar.copy(out=gates[:], in_=gate_bank[:])
 
-        relu = {}
+        last = PASSES - 1
+        first, second = slice(0, FIRST), slice(FIRST, C)
+        slot_plane = keep.tile([P, E * C], U8, name="slot_plane", align_bytes=64)
 
-        def expert_unit(e, n, bank, columns_of_slots, target):
-            width = columns_of_slots.stop - columns_of_slots.start
-            acc = psum.tile([P, width], F32, name=f"acc{e}_{n}_{columns_of_slots.start}", tag=f"bank{bank}")
+        def gather_plane(c):
+            nc.vector.tensor_copy(slot_plane[:, c], token_plane[:].indirect(lists(c)))
+
+        last_words = keep.tile([P, C], U32, name="last_words0", align_bytes=64)
+        slot_words[last, 0] = last_words[:]
+        for c in (first, second):
+            gather_plane(c)
+            nc.vector.tensor_copy(last_words[:, c], token_words[last][:].indirect(lists(c)))
+        gather_plane(slots(1))
+
+        products = [keep.tile([P, E * C], F32, name=f"products{n}") for n in range(N_TILES)]
+
+        def matmuls(n, bank, c):
+            e = c.start // C
+            own = slice(c.start - e * C, c.stop - e * C)
+            acc = psum.tile([P, c.stop - c.start], F32, name=f"acc{n}_{c.start}", tag=f"bank{bank}")
             tile, i = weights[e, n]
             for a in range(PASSES):
                 nc.tensor.matmul_mx(
                     out=acc[:],
                     lhsT=tile[:, a, i * P * PACK : (i + 1) * P * PACK].bitcast(FP8X4),
                     lhsT_scale=weight_planes[e][ROWS * a : P, n * P : (n + 1) * P],
-                    rhs=slot_words[a][:, columns_of_slots].bitcast(FP8X4),
-                    rhs_scale=slot_plane[ROWS * a : P, columns_of_slots],
+                    rhs=slot_words[a, e][:, own].bitcast(FP8X4),
+                    rhs_scale=slot_plane[ROWS * a : P, c],
                     start=(a == 0),
                     stop=(a == PASSES - 1),
                 )
-            nc.scalar.activation(out=target, in_=acc[:], func=RELU, bias=columns[:, e, n : n + 1])
+            return acc, columns[:, e, n : n + 1]
 
-        def whole_unit(e, n, bank):
-            relu[e, n] = keep.tile([P, C], F32, name=f"relu{e}_{n}")
-            expert_unit(e, n, bank, slots(e), relu[e, n][:])
+        relu = {}
 
-        def scatter_product(n, values, columns_of_slots):
-            nc.vector.tensor_tensor(windows[n][:].indirect(lists(columns_of_slots)), values, gates[:, columns_of_slots], MULT)
+        def relu_tile(n, c):
+            relu[n, c.start] = keep.tile([P, c.stop - c.start], F32, name=f"relu{n}_{c.start}", tag=f"relu{n}_{c.start}", align_bytes=64)
+            return relu[n, c.start][:]
+
+        def unit_on_scalar(n, bank, c):
+            acc, bias = matmuls(n, bank, c)
+            nc.scalar.activation(out=relu_tile(n, c), in_=acc[:], func=RELU, bias=bias)
+
+        def unit_on_vector(n, bank, c):
+            acc, bias = matmuls(n, bank, c)
+            nc.vector.tensor_scalar(relu_tile(n, c), acc[:], bias, 0.0, ADD, MAX)
+
+        def product(n, c):
+            nc.vector.tensor_tensor(products[n][:, c], relu[n, c.start][:], gate_bank[:, c], MULT)
+
+        def scatter_on_scalar(n, c):
+            nc.scalar.activation(out=windows[n][:].indirect(lists(c)), in_=products[n][:, c], func=COPY)
+
+        def scatter_on_vector(n, c):
+            nc.vector.tensor_copy(windows[n][:].indirect(lists(c)), products[n][:, c])
 
         def finish(n, lo, hi, engine, queue):
             result = keep.tile([P, hi - lo], F32, name=f"result{n}_{lo}")
             engine.tensor_tensor(result[:], windows[n][:, lo:hi], residuals[n][:, lo:hi], ADD)
             queue.dma_start(out=out[n * P : (n + 1) * P, lo:hi], in_=result[:])
 
-        first_relu = keep.tile([P, FIRST], F32, name="first_relu")
-        rest_relu = keep.tile([P, E * C - FIRST], F32, name="rest_relu")
-        expert_unit(0, 0, 0, slice(0, FIRST), first_relu[:])
-        scatter_product(0, first_relu[:], slice(0, FIRST))
-        for n in range(1, N_TILES - 1):
-            whole_unit(0, n, n + 1)
-            scatter_product(n, relu[0, n][:], slots(0))
-        expert_unit(0, 0, 4, slice(FIRST, C), rest_relu[:, : C - FIRST])
-        expert_unit(1, 0, 5, slots(1), rest_relu[:, C - FIRST :])
-        scatter_product(0, rest_relu[:], slice(FIRST, E * C))
-
-        products = {n: keep.tile([P, E * C], F32, name=f"products{n}") for n in range(1, N_TILES)}
-
-        def gate_product(e, tiles, turned_banks, back_banks):
-            turned = keep.tile([P, HALVES, len(tiles), P], F32, name=f"turned{e}_{tiles[0]}")
-            for h in range(HALVES):
-                bank = psum.tile([P, len(tiles), P], F32, name=f"turned_bank{e}_{tiles[0]}_{h}", tag=f"bank{turned_banks[h]}")
-                for i, n in enumerate(tiles):
-                    nc.tensor.transpose(bank[:, i, :], relu[e, n][:, h * P : (h + 1) * P], identity[:])
-                column = e * HALVES + h
-                nc.scalar.activation(
-                    out=turned[:, h, :, :], in_=bank[:], func=COPY, scale=gate_columns[:, column : column + 1]
-                )
-            for i, n in enumerate(tiles):
-                bank = psum.tile([P, C], F32, name=f"back_bank{e}_{n}", tag=f"bank{back_banks[i]}")
-                for h in range(HALVES):
-                    nc.tensor.transpose(bank[:, h * P : (h + 1) * P], turned[:, h, i, :], identity[:])
-                nc.scalar.copy(out=products[n][:, slots(e)], in_=bank[:])
-
-        for n, bank in ((1, 6), (2, 7), (3, 1)):
-            whole_unit(1, n, bank)
-        whole_unit(0, N_TILES - 1, 0)
-        gate_product(1, (1,), (2, 3), (4,))
-        gate_product(1, (2, 3), (5, 6), (7, 2))
-        gate_product(0, (3,), (3, 1), (4,))
-
-        finish(0, 0, T, nc.gpsimd, nc.sync)
-        for n in range(1, N_TILES - 1):
-            nc.vector.tensor_copy(windows[n][:].indirect(offsets[:, places(1)]), products[n][:, slots(1)])
-            if n < N_TILES - 2:
-                finish(n, 0, T, nc.gpsimd, nc.sync)
-        for lo in (0, T // 2):
-            finish(N_TILES - 2, lo, lo + T // 2, nc.gpsimd, nc.sync)
-        last = N_TILES - 1
-        nc.vector.tensor_copy(windows[last][:].indirect(offsets[:]), products[last][:])
-        for lo, queue in ((0, nc.sync), (T // 3, nc.scalar), (2 * T // 3, nc.sync)):
-            finish(last, lo, lo + T // 3, nc.vector, queue)
+        unit_on_scalar(0, 0, first)
+        unit_on_scalar(0, 2, second)
+        product(0, first)
+        last_words = keep.tile([P, C], U32, name="last_words1", tag="relu0_0", align_bytes=64)
+        slot_words[last, 1] = last_words[:]
+        nc.vector.tensor_copy(last_words[:], token_words[last][:].indirect(lists(slots(1))))
+        scatter_on_scalar(0, first)
+        product(0, second)
+        scatter_on_scalar(0, second)
+        for n, e, bank in ((1, 0, 3), (0, 1, 4), (1, 1, 5), (2, 0, 6), (3, 0, 7), (2, 1, 0), (3, 1, 2)):
+            unit_on_vector(n, bank, slots(e))
+            product(n, slots(e))
+            if n < 2:
+                scatter_on_scalar(n, slots(e))
+            elif n == 3:
+                scatter_on_vector(n, slots(e))
+            elif e == 0:
+                scatter_on_vector(n, first)
+            else:
+                scatter_on_scalar(n, slice(FIRST, E * C))
+        for n in (0, 1):
+            finish(n, 0, T, nc.gpsimd, nc.sync)
+        for n in (3, 2):
+            for lo in (0, T // 2):
+                finish(n, lo, lo + T // 2, nc.vector, nc.sync)

@@ -32,8 +32,9 @@ BYTES = 4 * K * T + 2 * 4 * N * T + E * K * N + E * (K // 32) * N + 4 * N * E + 
 WHOLE = ((0, T),)
 LOADS = (WHOLE, WHOLE, WHOLE, ((0, 256), (256, 512), (512, T)))
 HALF_EACH = ((0, 128, 128), (128, 256, 640), (640, T, T))
-GROUPS = (HALF_EACH, HALF_EACH, HALF_EACH, ((0, 256, 256), (256, 512, 512), (512, 640, T)))
+GROUPS = (HALF_EACH, HALF_EACH, HALF_EACH, ((0, 256, 256), (256, 384, 512), (512, 640, T)))
 FIRST = 128
+SHARE = 416
 
 
 def tile_moe_res_lin_relu_kernel(tc, xT, xr, w_words, w_scales, b, gate, offs, out):
@@ -84,7 +85,7 @@ def tile_moe_res_lin_relu_kernel(tc, xT, xr, w_words, w_scales, b, gate, offs, o
 
         def load_weights(e, tiles):
             words = w_words[e].rearrange("a p n r -> p a (n r)")[:, :, tiles[0] * P * PACK : (tiles[-1] + 1) * P * PACK]
-            tile = keep.tile([P, PASSES, len(tiles) * P * PACK], U8, name=f"weights{e}_{tiles[0]}", align_bytes=64)
+            tile = keep.tile([P, PASSES, len(tiles) * P * PACK], U8, name=f"weights{e}_{tiles[0]}", tag=f"weights{e}_{tiles[0]}", align_bytes=64)
             nc.sync.dma_start(out=tile[:].bitcast(I32), in_=words.bitcast(I32))
             for i, n in enumerate(tiles):
                 weights[e, n] = tile, i
@@ -98,12 +99,12 @@ def tile_moe_res_lin_relu_kernel(tc, xT, xr, w_words, w_scales, b, gate, offs, o
 
         load_scales(0)
         load_weights(0, (0, 1))
+        load_weights(0, (2, 3))
         load_scales(1)
         load_weights(1, (0, 1))
-        load_weights(0, (2, 3))
         load_weights(1, (2, 3))
         residuals = {}
-        for n in (0, 1, 3, 2):
+        for n in range(N_TILES):
             residuals[n] = keep.tile([P, T], F32, name=f"residual{n}")
             nc.sync.dma_start(out=residuals[n][:], in_=xr[n * P : (n + 1) * P, :])
 
@@ -144,11 +145,15 @@ def tile_moe_res_lin_relu_kernel(tc, xT, xr, w_words, w_scales, b, gate, offs, o
                 interleave_group(a, *group)
             for group in groups:
                 quantise_group(a, *group)
-            if a < PASSES - 1:
+            if a < PASSES - 2:
                 gathered = keep.tile([P, E * C], U32, name=f"slot_words{a}", align_bytes=64)
                 nc.vector.tensor_copy(gathered[:], token_words[a][:].indirect(offsets[:]))
                 for e in range(E):
                     slot_words[a, e] = gathered[:, slots(e)]
+            elif a == PASSES - 2:
+                gathered = keep.tile([P, C], U32, name=f"slot_words{a}", align_bytes=64)
+                nc.vector.tensor_copy(gathered[:], token_words[a][:].indirect(lists(slots(0))))
+                slot_words[a, 0] = gathered[:]
 
         column_bank = psum.tile([P, E + 1, P], F32, name="column_bank", tag="bank0")
         for e in range(E):
@@ -157,10 +162,16 @@ def tile_moe_res_lin_relu_kernel(tc, xT, xr, w_words, w_scales, b, gate, offs, o
         columns = keep.tile([P, E + 1, N_TILES], F32, name="columns", tag="raw0_0")
         nc.scalar.copy(out=columns[:], in_=column_bank[:, :, 0:N_TILES])
         gate_columns = columns[:, E, :]
+        first_bias = {}
+        for start in (0, FIRST):
+            first_bias[start] = keep.tile([P, 1], F32, name=f"first_bias{start}", tag=f"first_bias{start}", align_bytes=64)
+            nc.scalar.copy(out=first_bias[start][:], in_=column_bank[:, 0, 0:1])
 
         gate_bank = psum.tile([P, E * C], F32, name="gate_bank", tag="bank1")
         for i in range(E * HALVES):
             nc.tensor.transpose(gate_bank[:, i * P : (i + 1) * P], gate_columns[:, i : i + 1].to_broadcast([P, P]), identity[:])
+        gates = keep.tile([P, E * C], F32, name="gates", tag="raw1_0")
+        nc.scalar.copy(out=gates[:], in_=gate_bank[:])
 
         last = PASSES - 1
         first, second = slice(0, FIRST), slice(FIRST, C)
@@ -176,7 +187,7 @@ def tile_moe_res_lin_relu_kernel(tc, xT, xr, w_words, w_scales, b, gate, offs, o
             nc.vector.tensor_copy(last_words[:, c], token_words[last][:].indirect(lists(c)))
         gather_plane(slots(1))
 
-        products = [keep.tile([P, E * C], F32, name=f"products{n}") for n in range(N_TILES)]
+        products = {0: keep.tile([P, E * C], F32, name="products0")[:]}
 
         def matmuls(n, bank, c):
             e = c.start // C
@@ -193,7 +204,7 @@ def tile_moe_res_lin_relu_kernel(tc, xT, xr, w_words, w_scales, b, gate, offs, o
                     start=(a == 0),
                     stop=(a == PASSES - 1),
                 )
-            return acc, columns[:, e, n : n + 1]
+            return acc, first_bias[c.start][:] if (n, e) == (0, 0) else columns[:, e, n : n + 1]
 
         relu = {}
 
@@ -205,10 +216,6 @@ def tile_moe_res_lin_relu_kernel(tc, xT, xr, w_words, w_scales, b, gate, offs, o
             acc, bias = matmuls(n, bank, c)
             nc.scalar.activation(out=relu_tile(n, c), in_=acc[:], func=RELU, bias=bias)
 
-        def unit_on_vector(n, bank, c):
-            acc, bias = matmuls(n, bank, c)
-            nc.vector.tensor_scalar(relu_tile(n, c), acc[:], bias, 0.0, ADD, MAX)
-
         def product(n, c):
             nc.vector.tensor_tensor(products[n][:, c], relu[n, c.start][:], gate_bank[:, c], MULT)
 
@@ -218,6 +225,9 @@ def tile_moe_res_lin_relu_kernel(tc, xT, xr, w_words, w_scales, b, gate, offs, o
         def scatter_on_vector(n, c):
             nc.vector.tensor_copy(windows[n][:].indirect(lists(c)), products[n][:, c])
 
+        def scatter_product(n, c):
+            nc.vector.tensor_tensor(windows[n][:].indirect(lists(c)), relu[n, c.start][:], gates[:, c], MULT)
+
         def finish(n, lo, hi, engine, queue):
             result = keep.tile([P, hi - lo], F32, name=f"result{n}_{lo}")
             engine.tensor_tensor(result[:], windows[n][:, lo:hi], residuals[n][:, lo:hi], ADD)
@@ -226,25 +236,40 @@ def tile_moe_res_lin_relu_kernel(tc, xT, xr, w_words, w_scales, b, gate, offs, o
         unit_on_scalar(0, 0, first)
         unit_on_scalar(0, 2, second)
         product(0, first)
-        last_words = keep.tile([P, C], U32, name="last_words1", tag="relu0_0", align_bytes=64)
+        last_words = keep.tile([P, C], U32, name="last_words1", tag="first_bias0", align_bytes=64)
         slot_words[last, 1] = last_words[:]
         nc.vector.tensor_copy(last_words[:], token_words[last][:].indirect(lists(slots(1))))
         scatter_on_scalar(0, first)
         product(0, second)
+        put_off = keep.tile([P, C], U32, name="put_off_words", tag=f"first_bias{FIRST}", align_bytes=64)
+        slot_words[last - 1, 1] = put_off[:]
+        nc.vector.tensor_copy(put_off[:], token_words[last - 1][:].indirect(lists(slots(1))))
+        unit_on_scalar(1, 3, slots(0))
         scatter_on_scalar(0, second)
-        for n, e, bank in ((1, 0, 3), (0, 1, 4), (1, 1, 5), (2, 0, 6), (3, 0, 7), (2, 1, 0), (3, 1, 2)):
-            unit_on_vector(n, bank, slots(e))
-            product(n, slots(e))
-            if n < 2:
-                scatter_on_scalar(n, slots(e))
-            elif n == 3:
-                scatter_on_vector(n, slots(e))
-            elif e == 0:
-                scatter_on_vector(n, first)
-            else:
-                scatter_on_scalar(n, slice(FIRST, E * C))
+        scatter_product(1, slots(0))
+        unit_on_scalar(2, 4, slots(0))
+        unit_on_scalar(0, 6, slots(1))
+        unit_on_scalar(1, 7, slots(1))
+        unit_on_scalar(3, 6, slots(0))
+        product(0, slots(1))
+        scatter_on_scalar(0, slots(1))
+        scatter_product(1, slots(1))
+        unit_on_scalar(2, 0, slots(1))
+        last_acc, last_bias = matmuls(3, 2, slots(1))
+        late = keep.tile([P, 2, E * C], F32, name="late_products", tag="weights1_2", align_bytes=64)
+        for n in (2, 3):
+            products[n] = late[:, n - 2, :]
+        product(2, slots(0))
+        nc.vector.tensor_scalar(relu_tile(3, slots(1)), last_acc[:], last_bias, 0.0, ADD, MAX)
+        product(3, slots(0))
+        product(3, slots(1))
+        product(2, slots(1))
+        for e in range(E):
+            scatter_on_scalar(2, slots(e))
+        scatter_on_vector(3, slice(0, SHARE))
+        scatter_on_scalar(3, slice(SHARE, E * C))
         for n in (0, 1):
             finish(n, 0, T, nc.gpsimd, nc.sync)
-        for n in (3, 2):
+        for n in (2, 3):
             for lo in (0, T // 2):
                 finish(n, lo, lo + T // 2, nc.vector, nc.sync)

@@ -30,9 +30,9 @@ FLOPS = 2 * K * N * E * C
 BYTES = 4 * K * T + 2 * 4 * N * T + E * K * N + E * (K // 32) * N + 4 * N * E + 4 * E * C + 2 * P * E * LIST
 
 WHOLE = ((0, T),)
-LOADS = (WHOLE, WHOLE, WHOLE, ((0, 256), (256, 512), (512, T)))
+LOADS = (WHOLE, WHOLE, WHOLE, ((0, 512), (512, T)))
 HALF_EACH = ((0, 128, 128), (128, 256, 640), (640, T, T))
-GROUPS = (HALF_EACH, HALF_EACH, HALF_EACH, ((0, 256, 256), (256, 384, 512), (512, 640, T)))
+GROUPS = (HALF_EACH, HALF_EACH, HALF_EACH, ((0, 256, 256), (256, 384, 512), (512, 576, T)))
 FIRST = 128
 SHARE = 416
 

@@ -98,7 +98,8 @@ def tile_moe_res_lin_relu_kernel(tc, xT, xr, w_words, w_scales, b, gate, offs, o
                 )
 
         load_scales(0)
-        load_weights(0, (0, 1))
+        load_weights(0, (0,))
+        load_weights(0, (1,))
         load_weights(0, (2, 3))
         load_scales(1)
         load_weights(1, (0, 1))

@@ -34,6 +34,7 @@ LOADS = (WHOLE, WHOLE, WHOLE, ((0, 512), (512, T)))
 HALF_EACH = ((0, 128, 128), (128, 256, 640), (640, T, T))
 GROUPS = (HALF_EACH, HALF_EACH, HALF_EACH, ((0, 256, 256), (256, 384, 512), (512, 576, T)))
 FIRST = 128
+OPENING = 96
 SHARE = 416
 
 
@@ -240,13 +241,13 @@ def tile_moe_res_lin_relu_kernel(tc, xT, xr, w_words, w_scales, b, gate, offs, o
         last_words = keep.tile([P, C], U32, name="last_words1", tag="first_bias0", align_bytes=64)
         slot_words[last, 1] = last_words[:]
         nc.vector.tensor_copy(last_words[:], token_words[last][:].indirect(lists(slots(1))))
-        scatter_on_scalar(0, first)
+        scatter_on_scalar(0, slice(0, OPENING))
         product(0, second)
         put_off = keep.tile([P, C], U32, name="put_off_words", tag=f"first_bias{FIRST}", align_bytes=64)
         slot_words[last - 1, 1] = put_off[:]
         nc.vector.tensor_copy(put_off[:], token_words[last - 1][:].indirect(lists(slots(1))))
         unit_on_scalar(1, 3, slots(0))
-        scatter_on_scalar(0, second)
+        scatter_on_scalar(0, slice(OPENING, C))
         scatter_product(1, slots(0))
         unit_on_scalar(2, 4, slots(0))
         unit_on_scalar(0, 6, slots(1))

@@ -34,6 +34,7 @@ LOADS = (WHOLE, WHOLE, WHOLE, ((0, 512), (512, T)))
 HALF_EACH = ((0, 128, 128), (128, 256, 640), (640, T, T))
 GROUPS = (HALF_EACH, HALF_EACH, HALF_EACH, ((0, 256, 256), (256, 384, 512), (512, 576, T)))
 FIRST = 128
+WARM_UPS = 6
 OPENING = 96
 SHARE = 416
 
@@ -188,6 +189,20 @@ def tile_moe_res_lin_relu_kernel(tc, xT, xr, w_words, w_scales, b, gate, offs, o
             gather_plane(c)
             nc.vector.tensor_copy(last_words[:, c], token_words[last][:].indirect(lists(c)))
         gather_plane(slots(1))
+
+        warm_up = psum.tile([P, P], F32, name="warm_up", tag="bank5")
+        first_weights = weights[0, 0][0]
+        for step in range(WARM_UPS):
+            a = step % PASSES
+            nc.tensor.matmul_mx(
+                out=warm_up[:],
+                lhsT=first_weights[:, a, 0 : P * PACK].bitcast(FP8X4),
+                lhsT_scale=weight_planes[0][ROWS * a : P, 0:P],
+                rhs=first_weights[:, a, :].bitcast(FP8X4),
+                rhs_scale=weight_planes[0][ROWS * a : P, 0:P],
+                start=(step == 0),
+                stop=(step == WARM_UPS - 1),
+            )
 
         products = {0: keep.tile([P, E * C], F32, name="products0")[:]}
 

@@ -170,6 +170,9 @@ def tile_moe_res_lin_relu_kernel(tc, xT, xr, w_words, w_scales, b, gate, offs, o
             first_bias[start] = keep.tile([P, 1], F32, name=f"first_bias{start}", tag=f"first_bias{start}", align_bytes=64)
             nc.scalar.copy(out=first_bias[start][:], in_=column_bank[:, 0, 0:1])
 
+        held_bias = keep.tile([P, 1], F32, name="held_bias", tag="relu3_0", align_bytes=64)
+        nc.scalar.copy(out=held_bias[:], in_=column_bank[:, 1, 0:1])
+
         gate_bank = psum.tile([P, E * C], F32, name="gate_bank", tag="bank1")
         for i in range(E * HALVES):
             nc.tensor.transpose(gate_bank[:, i * P : (i + 1) * P], gate_columns[:, i : i + 1].to_broadcast([P, P]), identity[:])
@@ -221,6 +224,8 @@ def tile_moe_res_lin_relu_kernel(tc, xT, xr, w_words, w_scales, b, gate, offs, o
                     start=(a == 0),
                     stop=(a == PASSES - 1),
                 )
+            if (n, e) == (0, 1):
+                return acc, held_bias[:]
             return acc, first_bias[c.start][:] if (n, e) == (0, 0) else columns[:, e, n : n + 1]
 
         relu = {}
@@ -265,9 +270,10 @@ def tile_moe_res_lin_relu_kernel(tc, xT, xr, w_words, w_scales, b, gate, offs, o
         scatter_on_scalar(0, slice(OPENING, C))
         scatter_product(1, slots(0))
         unit_on_scalar(2, 4, slots(0))
+        early_acc, early_bias = matmuls(3, 5, slots(0))
         unit_on_scalar(0, 6, slots(1))
         unit_on_scalar(1, 7, slots(1))
-        unit_on_scalar(3, 6, slots(0))
+        nc.scalar.activation(out=relu_tile(3, slots(0)), in_=early_acc[:], func=RELU, bias=early_bias)
         product(0, slots(1))
         scatter_on_scalar(0, slots(1))
         scatter_product(1, slots(1))

@@ -9,7 +9,7 @@ PACK = 4
 K_PASS = P * PACK
 PASSES = K // K_PASS
 N_TILES = N // P
-LIST = C // 16
+SLOTS = E * C
 HALVES = C // P
 ROWS = 4
 
@@ -27,16 +27,11 @@ MULT = mybir.AluOpType.mult
 MAX = mybir.AluOpType.max
 
 FLOPS = 2 * K * N * E * C
-BYTES = 4 * K * T + 2 * 4 * N * T + E * K * N + E * (K // 32) * N + 4 * N * E + 4 * E * C + 2 * P * E * LIST
+BYTES = 4 * K * T + 2 * 4 * N * T + E * K * N + E * (K // 32) * N + 4 * N * E + 4 * E * C + 2 * P * SLOTS // 16
 
-WHOLE = ((0, T),)
-LOADS = (WHOLE, WHOLE, WHOLE, ((0, 512), (512, T)))
-HALF_EACH = ((0, 128, 128), (128, 256, 640), (640, T, T))
-GROUPS = (HALF_EACH, HALF_EACH, HALF_EACH, ((0, 256, 256), (256, 384, 512), (512, 576, T)))
-FIRST = 128
-WARM_UPS = 6
-OPENING = 96
-SHARE = 416
+SCALAR_BOTH = (None, 0, 0, 3)
+HELD = (None, None, 384, 128)
+SHARE = 352
 
 
 def tile_moe_res_lin_relu_kernel(tc, xT, xr, w_words, w_scales, b, gate, offs, out):
@@ -49,11 +44,10 @@ def tile_moe_res_lin_relu_kernel(tc, xT, xr, w_words, w_scales, b, gate, offs, o
         def slots(e):
             return slice(e * C, (e + 1) * C)
 
-        def places(e):
-            return slice(e * LIST, (e + 1) * LIST)
-
-        short_rows = keep.tile([P, (E + 1) * P], F32, name="short_rows")
-        nc.gpsimd.memset(short_rows[:], 0.0)
+        bias_rows = keep.tile([P, E * P], F32, name="bias_rows")
+        nc.vector.memset(bias_rows[:], 0.0)
+        gate_rows = keep.tile([P, P], F32, name="gate_rows")
+        nc.vector.memset(gate_rows[:], 0.0)
         identity = keep.tile([P, P], F32, name="identity")
         make_identity(nc, identity[:])
 
@@ -62,26 +56,27 @@ def tile_moe_res_lin_relu_kernel(tc, xT, xr, w_words, w_scales, b, gate, offs, o
             plane = keep.tile([P, N], U8, name=f"weight_plane{e}", align_bytes=64)
             nc.vector.memset(plane[:].bitcast(I32), 0)
             weight_planes.append(plane)
-        token_plane = keep.tile([P, T], U8, name="token_plane", align_bytes=64)
-        nc.vector.memset(token_plane[:].bitcast(I32), 0)
 
         windows = []
         for n in range(N_TILES):
             window = keep.tile([P, T], F32, name=f"window{n}")
-            nc.vector.memset(window[:], 0.0)
+            if n == 2:
+                nc.scalar.copy(out=window[:], in_=windows[0][:])
+            else:
+                nc.vector.memset(window[:], 0.0)
             windows.append(window)
 
-        offsets = keep.tile([P, E * LIST], U16, name="offsets")
+        offsets = keep.tile([P, SLOTS // 16], U16, name="offsets")
+        nc.sync.dma_start(offsets[:], offs)
         raw = {}
         for a in range(PASSES):
             rows = xT[a * K_PASS : (a + 1) * K_PASS, :].rearrange("(p j) t -> p j t", j=PACK)
-            for lo, hi in LOADS[a]:
-                raw[a, lo] = keep.tile([P, PACK, hi - lo], F32, name=f"raw{a}_{lo}", tag=f"raw{a}_{lo}")
-                nc.sync.dma_start(out=raw[a, lo][:], in_=rows[:, :, lo:hi])
-            if a == 0:
-                nc.sync.dma_start(offsets[:], offs)
-                nc.sync.dma_start(out=short_rows[0:N_TILES, 0 : E * P], in_=b.rearrange("(n p) e -> n (p e)", p=P))
-                nc.sync.dma_start(out=short_rows[0:N_TILES, E * P :], in_=gate[0, :].rearrange("(n p) -> n p", p=P))
+            for j in range(PACK):
+                raw[a, j] = keep.tile([P, T], F32, name=f"raw{a}_{j}", tag=f"raw{a}_{j}", align_bytes=64)
+                nc.sync.dma_start(out=raw[a, j][:], in_=rows[:, j, :])
+                if (a, j) == (0, 0):
+                    nc.sync.dma_start(out=bias_rows[0:N_TILES, :], in_=b.rearrange("(n p) e -> n (p e)", p=P))
+                    nc.sync.dma_start(out=gate_rows[0:N_TILES, :], in_=gate[0, :].rearrange("(n p) -> n p", p=P))
 
         weights = {}
 
@@ -102,197 +97,181 @@ def tile_moe_res_lin_relu_kernel(tc, xT, xr, w_words, w_scales, b, gate, offs, o
         load_scales(0)
         load_weights(0, (0,))
         load_weights(0, (1,))
-        load_weights(0, (2, 3))
+        gates = keep.tile([P, SLOTS], F32, name="gates")
+        nc.sync.dma_start(out=gates[:], in_=gate[0:P, :])
+        load_weights(0, (2,))
         load_scales(1)
         load_weights(1, (0, 1))
+        load_weights(0, (3,))
         load_weights(1, (2, 3))
         residuals = {}
         for n in range(N_TILES):
-            residuals[n] = keep.tile([P, T], F32, name=f"residual{n}")
+            residuals[n] = keep.tile([P, T], F32, name=f"residual{n}", tag=f"residual{n}")
             nc.sync.dma_start(out=residuals[n][:], in_=xr[n * P : (n + 1) * P, :])
-
-        token_words = []
-        slot_words = {}
-
-        def interleave(a, grouped, lo, first, last, copy):
-            if first < last:
-                start = max(piece[0] for piece in LOADS[a] if piece[0] <= first)
-                copy(
-                    out=grouped[:, first - lo : last - lo, :].rearrange("p (c i) j -> p c j i", i=2),
-                    in_=raw[a, start][:, :, first - start : last - start].rearrange("p j (c i) -> p c j i", i=2),
-                )
-
-        grouped = {}
-
-        def interleave_group(a, lo, mid, hi):
-            tile = keep.tile([P, hi - lo, PACK], BF16, name=f"grouped{a}_{lo}", tag=f"grouped{a}_{lo}", align_bytes=64)
-            interleave(a, tile, lo, lo, mid, nc.scalar.copy)
-            interleave(a, tile, lo, mid, hi, nc.vector.tensor_copy)
-            grouped[a, lo] = tile
-
-        def quantise_group(a, lo, mid, hi):
-            nc.vector.quantize_mx(
-                out=token_words[a][:, lo:hi].bitcast(FP8X4),
-                scales=token_plane[ROWS * a : P, lo:hi],
-                in_=grouped[a, lo][:].rearrange("p t j -> p (t j)"),
-            )
-
-        for a in range(PASSES):
-            token_words.append(keep.tile([P, T], U32, name=f"token_words{a}", align_bytes=64))
-        def lists(columns):
-            return offsets[:, columns.start // 16 : columns.stop // 16]
-
-        for a in range(PASSES):
-            groups = GROUPS[a]
-            for group in groups:
-                interleave_group(a, *group)
-            for group in groups:
-                quantise_group(a, *group)
-            if a < PASSES - 2:
-                gathered = keep.tile([P, E * C], U32, name=f"slot_words{a}", align_bytes=64)
-                nc.vector.tensor_copy(gathered[:], token_words[a][:].indirect(offsets[:]))
-                for e in range(E):
-                    slot_words[a, e] = gathered[:, slots(e)]
-            elif a == PASSES - 2:
-                gathered = keep.tile([P, C], U32, name=f"slot_words{a}", align_bytes=64)
-                nc.vector.tensor_copy(gathered[:], token_words[a][:].indirect(lists(slots(0))))
-                slot_words[a, 0] = gathered[:]
 
         column_bank = psum.tile([P, E + 1, P], F32, name="column_bank", tag="bank0")
         for e in range(E):
-            nc.tensor.transpose(column_bank[:, e, :], short_rows[:, e : E * P : E], identity[:])
-        nc.tensor.transpose(column_bank[:, E, :], short_rows[:, E * P :], identity[:])
-        columns = keep.tile([P, E + 1, N_TILES], F32, name="columns", tag="raw0_0")
-        nc.scalar.copy(out=columns[:], in_=column_bank[:, :, 0:N_TILES])
+            nc.tensor.transpose(column_bank[:, e, :], bias_rows[:, e : E * P : E], identity[:])
+        nc.tensor.transpose(column_bank[:, E, :], gate_rows[:], identity[:])
+        columns = keep.tile([P, E + 1, N_TILES], F32, name="columns")
+        nc.vector.tensor_copy(out=columns[:], in_=column_bank[:, :, 0:N_TILES])
         gate_columns = columns[:, E, :]
-        first_bias = {}
-        for start in (0, FIRST):
-            first_bias[start] = keep.tile([P, 1], F32, name=f"first_bias{start}", tag=f"first_bias{start}", align_bytes=64)
-            nc.scalar.copy(out=first_bias[start][:], in_=column_bank[:, 0, 0:1])
-
-        held_bias = keep.tile([P, 1], F32, name="held_bias", tag="relu3_0", align_bytes=64)
-        nc.scalar.copy(out=held_bias[:], in_=column_bank[:, 1, 0:1])
-
-        gate_bank = psum.tile([P, E * C], F32, name="gate_bank", tag="bank1")
+        biases = {(n, e): columns[:, e, n : n + 1] for n in range(N_TILES) for e in range(E)}
+        gate_bank = psum.tile([P, SLOTS], F32, name="gate_bank", tag="bank1")
         for i in range(E * HALVES):
             nc.tensor.transpose(gate_bank[:, i * P : (i + 1) * P], gate_columns[:, i : i + 1].to_broadcast([P, P]), identity[:])
-        gates = keep.tile([P, E * C], F32, name="gates", tag="raw1_0")
-        nc.scalar.copy(out=gates[:], in_=gate_bank[:])
 
+        def lists(c):
+            return offsets[:, c.start // 16 : c.stop // 16]
+
+        def gather_on_vector(dst, a, j, c):
+            nc.vector.tensor_copy(dst, raw[a, j][:].indirect(lists(c)))
+
+        def gather_on_scalar(dst, a, j, c):
+            nc.scalar.activation(out=dst, in_=raw[a, j][:].indirect(lists(c)), func=COPY)
+
+        grouped, slot_words, slot_planes = {}, {}, {}
         last = PASSES - 1
-        first, second = slice(0, FIRST), slice(FIRST, C)
-        slot_plane = keep.tile([P, E * C], U8, name="slot_plane", align_bytes=64)
+        picked = {}
+        for a in range(PASSES):
+            picked[a, 1] = keep.tile([P, (PACK + 1) * C], F32, name=f"picked{a}_1", align_bytes=64)[:]
+        for a in range(PASSES):
+            if a == 0:
+                picked[a, 0] = picked[1, 1][:, C:]
+            else:
+                picked[a, 0] = keep.tile([P, PACK * C], F32, name=f"picked{a}_0", tag=f"picked{a}_0", align_bytes=64)[:]
+        for a in range(PASSES):
+            picked[a, 1] = picked[a, 1][:, 0 : PACK * C]
 
-        def gather_plane(c):
-            nc.vector.tensor_copy(slot_plane[:, c], token_plane[:].indirect(lists(c)))
-
-        last_words = keep.tile([P, C], U32, name="last_words0", align_bytes=64)
-        slot_words[last, 0] = last_words[:]
-        for c in (first, second):
-            gather_plane(c)
-            nc.vector.tensor_copy(last_words[:, c], token_words[last][:].indirect(lists(c)))
-        gather_plane(slots(1))
-
-        warm_up = psum.tile([P, P], F32, name="warm_up", tag="bank5")
-        first_weights = weights[0, 0][0]
-        for step in range(WARM_UPS):
-            a = step % PASSES
-            nc.tensor.matmul_mx(
-                out=warm_up[:],
-                lhsT=first_weights[:, a, 0 : P * PACK].bitcast(FP8X4),
-                lhsT_scale=weight_planes[0][ROWS * a : P, 0:P],
-                rhs=first_weights[:, a, :].bitcast(FP8X4),
-                rhs_scale=weight_planes[0][ROWS * a : P, 0:P],
-                start=(step == 0),
-                stop=(step == WARM_UPS - 1),
+        def interleave(a, e, copy):
+            copy(
+                out=grouped[a, e].rearrange("p (c i j) -> p c j i", i=2, j=PACK),
+                in_=picked[a, e].rearrange("p (j c i) -> p c j i", i=2, j=PACK),
             )
 
-        products = {0: keep.tile([P, E * C], F32, name="products0")[:]}
+        def quantise(a, e, tag):
+            slot_words[a, e] = keep.tile([P, C], U32, name=f"slot_words{a}_{e}", tag=tag, align_bytes=64)
+            slot_planes[a, e] = keep.tile([P, C], U8, name=f"slot_plane{a}_{e}", align_bytes=64)
+            nc.vector.quantize_mx(out=slot_words[a, e][:].bitcast(FP8X4), scales=slot_planes[a, e][:], in_=grouped[a, e])
 
-        def matmuls(n, bank, c):
-            e = c.start // C
-            own = slice(c.start - e * C, c.stop - e * C)
-            acc = psum.tile([P, c.stop - c.start], F32, name=f"acc{n}_{c.start}", tag=f"bank{bank}")
+        for a in range(PASSES):
+            for j in range(PACK):
+                for e in range(E):
+                    gather = gather_on_vector if e == 1 and j != SCALAR_BOTH[a] else gather_on_scalar
+                    gather(picked[a, e][:, j * C : (j + 1) * C], a, j, slots(e))
+            if a + 2 < PASSES:
+                grouped[a, 0] = picked[a + 2, 1][:, HELD[a + 2] : HELD[a + 2] + 2 * C].bitcast(BF16)
+            else:
+                grouped[a, 0] = keep.tile([P, C * PACK], BF16, name=f"grouped{a}_0", align_bytes=64)[:]
+            interleave(a, 0, nc.vector.tensor_copy)
+            if a > 0:
+                quantise(a - 1, 1, f"raw{a}_3")
+            quantise(a, 0, f"words{a}")
+            if a < last:
+                grouped[a, 1] = grouped[a, 0]
+                nc.gpsimd.tensor_copy(
+                    out=grouped[a, 1].rearrange("p (t j) -> p t j", j=PACK),
+                    in_=picked[a, 1].rearrange("p (j t) -> p t j", j=PACK),
+                )
+            else:
+                grouped[a, 1] = keep.tile([P, C * PACK], BF16, name="last_grouped1", align_bytes=64)[:]
+                interleave(a, 1, nc.scalar.copy)
+                quantise(a, 1, "last_words")
+
+        sums, relu, products = {}, {}, {}
+
+        def open_bank(bank, *units):
+            tile = psum.tile([P, len(units) * C], F32, name=f"sums{units[0][0]}_{units[0][1]}", tag=f"bank{bank}")
+            for i, unit in enumerate(units):
+                sums[unit] = tile[:, i * C : (i + 1) * C]
+
+        def matmuls(n, e, passes=range(PASSES), opens=True, closes=True):
             tile, i = weights[e, n]
-            for a in range(PASSES):
+            for a in passes:
                 nc.tensor.matmul_mx(
-                    out=acc[:],
+                    out=sums[n, e],
                     lhsT=tile[:, a, i * P * PACK : (i + 1) * P * PACK].bitcast(FP8X4),
                     lhsT_scale=weight_planes[e][ROWS * a : P, n * P : (n + 1) * P],
-                    rhs=slot_words[a, e][:, own].bitcast(FP8X4),
-                    rhs_scale=slot_plane[ROWS * a : P, c],
-                    start=(a == 0),
-                    stop=(a == PASSES - 1),
+                    rhs=slot_words[a, e][:].bitcast(FP8X4),
+                    rhs_scale=slot_planes[a, e][:],
+                    start=(opens and a == 0),
+                    stop=(closes and a == last),
                 )
-            if (n, e) == (0, 1):
-                return acc, held_bias[:]
-            return acc, first_bias[c.start][:] if (n, e) == (0, 0) else columns[:, e, n : n + 1]
 
-        relu = {}
+        def room(tag, width=C):
+            return keep.tile([P, width], F32, name=f"on_{tag}", tag=tag)[:]
 
-        def relu_tile(n, c):
-            relu[n, c.start] = keep.tile([P, c.stop - c.start], F32, name=f"relu{n}_{c.start}", tag=f"relu{n}_{c.start}", align_bytes=64)
-            return relu[n, c.start][:]
+        def relu_on_scalar(n, e, dst):
+            relu[n, e] = dst
+            nc.scalar.activation(out=dst, in_=sums[n, e], func=RELU, bias=biases[n, e])
 
-        def unit_on_scalar(n, bank, c):
-            acc, bias = matmuls(n, bank, c)
-            nc.scalar.activation(out=relu_tile(n, c), in_=acc[:], func=RELU, bias=bias)
+        def relu_on_vector(n, e, dst):
+            relu[n, e] = dst
+            nc.vector.tensor_scalar(dst, sums[n, e], biases[n, e], 0.0, ADD, MAX)
 
-        def product(n, c):
-            nc.vector.tensor_tensor(products[n][:, c], relu[n, c.start][:], gate_bank[:, c], MULT)
+        def product(n, e, dst):
+            products[n, e] = dst
+            nc.vector.tensor_tensor(dst, relu[n, e], gate_bank[:, slots(e)], MULT)
 
-        def scatter_on_scalar(n, c):
-            nc.scalar.activation(out=windows[n][:].indirect(lists(c)), in_=products[n][:, c], func=COPY)
+        def own(e, c):
+            return slice(c.start - e * C, c.stop - e * C)
 
-        def scatter_on_vector(n, c):
-            nc.vector.tensor_copy(windows[n][:].indirect(lists(c)), products[n][:, c])
+        def scatter_on_scalar(n, e, c):
+            nc.scalar.activation(out=windows[n][:].indirect(lists(c)), in_=products[n, e][:, own(e, c)], func=COPY)
 
-        def scatter_product(n, c):
-            nc.vector.tensor_tensor(windows[n][:].indirect(lists(c)), relu[n, c.start][:], gates[:, c], MULT)
+        def scatter_on_vector(n, e, c):
+            nc.vector.tensor_copy(windows[n][:].indirect(lists(c)), products[n, e][:, own(e, c)])
 
-        def finish(n, lo, hi, engine, queue):
-            result = keep.tile([P, hi - lo], F32, name=f"result{n}_{lo}")
-            engine.tensor_tensor(result[:], windows[n][:, lo:hi], residuals[n][:, lo:hi], ADD)
-            queue.dma_start(out=out[n * P : (n + 1) * P, lo:hi], in_=result[:])
+        def scatter_product(n, e):
+            nc.vector.tensor_tensor(windows[n][:].indirect(lists(slots(e))), relu[n, e], gates[:, slots(e)], MULT)
 
-        unit_on_scalar(0, 0, first)
-        unit_on_scalar(0, 2, second)
-        product(0, first)
-        last_words = keep.tile([P, C], U32, name="last_words1", tag="first_bias0", align_bytes=64)
-        slot_words[last, 1] = last_words[:]
-        nc.vector.tensor_copy(last_words[:], token_words[last][:].indirect(lists(slots(1))))
-        scatter_on_scalar(0, slice(0, OPENING))
-        product(0, second)
-        put_off = keep.tile([P, C], U32, name="put_off_words", tag=f"first_bias{FIRST}", align_bytes=64)
-        slot_words[last - 1, 1] = put_off[:]
-        nc.vector.tensor_copy(put_off[:], token_words[last - 1][:].indirect(lists(slots(1))))
-        unit_on_scalar(1, 3, slots(0))
-        scatter_on_scalar(0, slice(OPENING, C))
-        scatter_product(1, slots(0))
-        unit_on_scalar(2, 4, slots(0))
-        early_acc, early_bias = matmuls(3, 5, slots(0))
-        unit_on_scalar(0, 6, slots(1))
-        unit_on_scalar(1, 7, slots(1))
-        nc.scalar.activation(out=relu_tile(3, slots(0)), in_=early_acc[:], func=RELU, bias=early_bias)
-        product(0, slots(1))
-        scatter_on_scalar(0, slots(1))
-        scatter_product(1, slots(1))
-        unit_on_scalar(2, 0, slots(1))
-        last_acc, last_bias = matmuls(3, 2, slots(1))
-        late = keep.tile([P, 2, E * C], F32, name="late_products", tag="weights1_2", align_bytes=64)
-        for n in (2, 3):
-            products[n] = late[:, n - 2, :]
-        product(2, slots(0))
-        nc.vector.tensor_scalar(relu_tile(3, slots(1)), last_acc[:], last_bias, 0.0, ADD, MAX)
-        product(3, slots(0))
-        product(3, slots(1))
-        product(2, slots(1))
-        for e in range(E):
-            scatter_on_scalar(2, slots(e))
-        scatter_on_vector(3, slice(0, SHARE))
-        scatter_on_scalar(3, slice(SHARE, E * C))
+        def finish(n, lo, hi, engine, result):
+            engine.tensor_tensor(result[:, lo:hi], windows[n][:, lo:hi], residuals[n][:, lo:hi], ADD)
+            nc.sync.dma_start(out=out[n * P : (n + 1) * P, lo:hi], in_=result[:, lo:hi])
+
+        ring = room("ring", 2 * C)
+        low, middle, high = ring[:, 0:C], ring[:, C // 2 : C // 2 + C], ring[:, C:]
+        open_bank(0, (0, 0), (1, 0))
+        for passes in (range(last), (last,)):
+            matmuls(0, 0, passes, closes=False)
+            matmuls(1, 0, passes, opens=False)
+        relu_on_scalar(0, 0, middle)
+        relu_on_scalar(1, 0, room("relu10"))
+        open_bank(2, (2, 0))
+        open_bank(0, (0, 1), (1, 1))
+        matmuls(2, 0)
+        matmuls(0, 1)
+        matmuls(1, 1)
+        product(0, 0, room("product00"))
+        scatter_on_scalar(0, 0, slots(0))
+        scatter_product(1, 0)
+        relu_on_vector(2, 0, room("relu20"))
+        relu_on_scalar(0, 1, low)
+        relu_on_scalar(1, 1, high)
+        open_bank(2, (3, 0))
+        open_bank(0, (2, 1), (3, 1))
+        matmuls(3, 0)
+        matmuls(2, 1)
+        matmuls(3, 1)
+        late = keep.tile([P, 2 * C], F32, name="late", tag="weights1_2", align_bytes=64)
+        product(0, 1, room("product01"))
+        scatter_on_scalar(0, 1, slots(1))
+        scatter_product(1, 1)
+        product(2, 0, late[:, 0:C])
+        relu_on_scalar(3, 0, low)
+        scatter_on_scalar(2, 0, slots(0))
+        relu_on_vector(2, 1, room("relu21"))
+        product(3, 0, late[:, C:])
+        product(2, 1, room("product21"))
+        scatter_on_vector(3, 0, slots(0))
+        relu_on_scalar(3, 1, room("relu20"))
+        scatter_on_scalar(2, 1, slots(1))
+        product(3, 1, low)
+        scatter_on_vector(3, 1, slice(C, SHARE))
+        scatter_on_scalar(3, 1, slice(SHARE, SLOTS))
         for n in (0, 1):
-            finish(n, 0, T, nc.gpsimd, nc.sync)
+            finish(n, 0, T, nc.gpsimd, room(f"result{n}", T))
         for n in (2, 3):
+            result = room(("relu20", "result3")[n - 2], T)
             for lo in (0, T // 2):
-                finish(n, lo, lo + T // 2, nc.vector, nc.sync)
+                finish(n, lo, lo + T // 2, nc.vector, result)

@@ -29,8 +29,7 @@ MAX = mybir.AluOpType.max
 FLOPS = 2 * K * N * E * C
 BYTES = 4 * K * T + 2 * 4 * N * T + E * K * N + E * (K // 32) * N + 4 * N * E + 4 * E * C + 2 * P * SLOTS // 16
 
-SCALAR_BOTH = (None, 0, 0, 3)
-HELD = (None, None, 384, 128)
+HELD = 384
 SHARE = 352
 
 
@@ -39,6 +38,7 @@ def tile_moe_res_lin_relu_kernel(tc, xT, xr, w_words, w_scales, b, gate, offs, o
 
     with ExitStack() as ctx:
         keep = ctx.enter_context(tc.tile_pool(name="keep", bufs=1))
+        shared = ctx.enter_context(tc.tile_pool(name="shared", bufs=1))
         psum = ctx.enter_context(tc.psum_pool(name="psum", bufs=1))
 
         def slots(e):
@@ -80,12 +80,15 @@ def tile_moe_res_lin_relu_kernel(tc, xT, xr, w_words, w_scales, b, gate, offs, o
 
         weights = {}
 
-        def load_weights(e, tiles):
-            words = w_words[e].rearrange("a p n r -> p a (n r)")[:, :, tiles[0] * P * PACK : (tiles[-1] + 1) * P * PACK]
-            tile = keep.tile([P, PASSES, len(tiles) * P * PACK], U8, name=f"weights{e}_{tiles[0]}", tag=f"weights{e}_{tiles[0]}", align_bytes=64)
+        def load_weights(e, tiles, passes=range(PASSES)):
+            width = len(tiles) * P * PACK
+            words = w_words[e].rearrange("a p n r -> p a (n r)")[:, passes.start : passes.stop, tiles[0] * P * PACK : tiles[0] * P * PACK + width]
+            name = f"weights{e}_{tiles[0]}_{passes.start}"
+            tile = keep.tile([P, len(passes), width], U8, name=name, tag=name, align_bytes=64)
             nc.sync.dma_start(out=tile[:].bitcast(I32), in_=words.bitcast(I32))
             for i, n in enumerate(tiles):
-                weights[e, n] = tile, i
+                for a in passes:
+                    weights[e, n, a] = tile[:, a - passes.start, i * P * PACK : (i + 1) * P * PACK]
 
         def load_scales(e):
             for quadrant in range(4):
@@ -95,13 +98,11 @@ def tile_moe_res_lin_relu_kernel(tc, xT, xr, w_words, w_scales, b, gate, offs, o
                 )
 
         load_scales(0)
-        load_weights(0, (0,))
-        load_weights(0, (1,))
-        gates = keep.tile([P, SLOTS], F32, name="gates")
-        nc.sync.dma_start(out=gates[:], in_=gate[0:P, :])
-        load_weights(0, (2,))
+        for passes in (range(0, 1), range(1, 2), range(2, PASSES)):
+            load_weights(0, (0, 1), passes)
         load_scales(1)
         load_weights(1, (0, 1))
+        load_weights(0, (2,))
         load_weights(0, (3,))
         load_weights(1, (2, 3))
         residuals = {}
@@ -138,6 +139,8 @@ def tile_moe_res_lin_relu_kernel(tc, xT, xr, w_words, w_scales, b, gate, offs, o
         for a in range(PASSES):
             if a == 0:
                 picked[a, 0] = picked[1, 1][:, C:]
+            elif a == last:
+                picked[a, 0] = shared.tile([P, PACK * C], F32, name="last_picked", align_bytes=64, offset=0)[:]
             else:
                 picked[a, 0] = keep.tile([P, PACK * C], F32, name=f"picked{a}_0", tag=f"picked{a}_0", align_bytes=64)[:]
         for a in range(PASSES):
@@ -150,21 +153,30 @@ def tile_moe_res_lin_relu_kernel(tc, xT, xr, w_words, w_scales, b, gate, offs, o
             )
 
         def quantise(a, e, tag):
-            slot_words[a, e] = keep.tile([P, C], U32, name=f"slot_words{a}_{e}", tag=tag, align_bytes=64)
+            if tag is None:
+                slot_words[a, e] = shared.tile([P, C], U32, name="late_words", align_bytes=64, offset=0)
+            else:
+                slot_words[a, e] = keep.tile([P, C], U32, name=f"slot_words{a}_{e}", tag=tag, align_bytes=64)
             slot_planes[a, e] = keep.tile([P, C], U8, name=f"slot_plane{a}_{e}", align_bytes=64)
             nc.vector.quantize_mx(out=slot_words[a, e][:].bitcast(FP8X4), scales=slot_planes[a, e][:], in_=grouped[a, e])
 
         for a in range(PASSES):
             for j in range(PACK):
-                for e in range(E):
-                    gather = gather_on_vector if e == 1 and j != SCALAR_BOTH[a] else gather_on_scalar
-                    gather(picked[a, e][:, j * C : (j + 1) * C], a, j, slots(e))
+                row = [picked[a, e][:, j * C : (j + 1) * C] for e in range(E)]
+                if (a, j) == (last, PACK - 1):
+                    gather_on_scalar(row[0][:, 0 : C // 2], a, j, slice(0, C // 2))
+                    gather_on_vector(row[0][:, C // 2 :], a, j, slice(C // 2, C))
+                    gather_on_scalar(row[1], a, j, slots(1))
+                else:
+                    gather_on_scalar(row[0], a, j, slots(0))
+                    gather = gather_on_scalar if j == 0 and a > 0 else gather_on_vector
+                    gather(row[1], a, j, slots(1))
             if a + 2 < PASSES:
-                grouped[a, 0] = picked[a + 2, 1][:, HELD[a + 2] : HELD[a + 2] + 2 * C].bitcast(BF16)
+                grouped[a, 0] = picked[a + 2, 1][:, HELD : HELD + 2 * C].bitcast(BF16)
             else:
                 grouped[a, 0] = keep.tile([P, C * PACK], BF16, name=f"grouped{a}_0", align_bytes=64)[:]
             interleave(a, 0, nc.vector.tensor_copy)
-            if a > 0:
+            if 0 < a < last:
                 quantise(a - 1, 1, f"raw{a}_3")
             quantise(a, 0, f"words{a}")
             if a < last:
@@ -174,7 +186,10 @@ def tile_moe_res_lin_relu_kernel(tc, xT, xr, w_words, w_scales, b, gate, offs, o
                     in_=picked[a, 1].rearrange("p (j t) -> p t j", j=PACK),
                 )
             else:
-                grouped[a, 1] = keep.tile([P, C * PACK], BF16, name="last_grouped1", align_bytes=64)[:]
+                grouped[a, 1] = shared.tile([P, C * PACK], BF16, name="last_grouped1", align_bytes=64, offset=4 * C * PACK)[:]
+                quantise(a - 1, 1, None)
+                gates = shared.tile([P, SLOTS], F32, name="gates", align_bytes=64, offset=4 * C)
+                nc.vector.tensor_copy(out=gates[:], in_=gate_bank[:])
                 interleave(a, 1, nc.scalar.copy)
                 quantise(a, 1, "last_words")
 
@@ -186,11 +201,10 @@ def tile_moe_res_lin_relu_kernel(tc, xT, xr, w_words, w_scales, b, gate, offs, o
                 sums[unit] = tile[:, i * C : (i + 1) * C]
 
         def matmuls(n, e, passes=range(PASSES), opens=True, closes=True):
-            tile, i = weights[e, n]
             for a in passes:
                 nc.tensor.matmul_mx(
                     out=sums[n, e],
-                    lhsT=tile[:, a, i * P * PACK : (i + 1) * P * PACK].bitcast(FP8X4),
+                    lhsT=weights[e, n, a].bitcast(FP8X4),
                     lhsT_scale=weight_planes[e][ROWS * a : P, n * P : (n + 1) * P],
                     rhs=slot_words[a, e][:].bitcast(FP8X4),
                     rhs_scale=slot_planes[a, e][:],
@@ -232,13 +246,13 @@ def tile_moe_res_lin_relu_kernel(tc, xT, xr, w_words, w_scales, b, gate, offs, o
         ring = room("ring", 2 * C)
         low, middle, high = ring[:, 0:C], ring[:, C // 2 : C // 2 + C], ring[:, C:]
         open_bank(0, (0, 0), (1, 0))
-        for passes in (range(last), (last,)):
-            matmuls(0, 0, passes, closes=False)
-            matmuls(1, 0, passes, opens=False)
+        for a in range(PASSES):
+            matmuls(0, 0, (a,), closes=False)
+            matmuls(1, 0, (a,), opens=False)
         relu_on_scalar(0, 0, middle)
         relu_on_scalar(1, 0, room("relu10"))
-        open_bank(2, (2, 0))
-        open_bank(0, (0, 1), (1, 1))
+        open_bank(0, (2, 0))
+        open_bank(2, (0, 1), (1, 1))
         matmuls(2, 0)
         matmuls(0, 1)
         matmuls(1, 1)
@@ -248,12 +262,12 @@ def tile_moe_res_lin_relu_kernel(tc, xT, xr, w_words, w_scales, b, gate, offs, o
         relu_on_vector(2, 0, room("relu20"))
         relu_on_scalar(0, 1, low)
         relu_on_scalar(1, 1, high)
-        open_bank(2, (3, 0))
-        open_bank(0, (2, 1), (3, 1))
+        open_bank(0, (3, 0))
+        open_bank(2, (2, 1), (3, 1))
         matmuls(3, 0)
         matmuls(2, 1)
         matmuls(3, 1)
-        late = keep.tile([P, 2 * C], F32, name="late", tag="weights1_2", align_bytes=64)
+        late = keep.tile([P, 2 * C], F32, name="late", tag="weights1_2_0", align_bytes=64)
         product(0, 1, room("product01"))
         scatter_on_scalar(0, 1, slots(1))
         scatter_product(1, 1)

@@ -29,6 +29,7 @@ MAX = mybir.AluOpType.max
 FLOPS = 2 * K * N * E * C
 BYTES = 4 * K * T + 2 * 4 * N * T + E * K * N + E * (K // 32) * N + 4 * N * E + 4 * E * C + 2 * P * SLOTS // 16
 
+ON_VECTOR = (((0, 1), (1, 1), (2, 1), (3, 1)), ((1, 1), (2, 1), (3, 1)), ((1, 1), (2, 1), (3, 1)), ((1, 1), (3, 0)))
 HELD = 384
 SHARE = 352
 
@@ -70,10 +71,11 @@ def tile_moe_res_lin_relu_kernel(tc, xT, xr, w_words, w_scales, b, gate, offs, o
         nc.sync.dma_start(offsets[:], offs)
         raw = {}
         for a in range(PASSES):
-            rows = xT[a * K_PASS : (a + 1) * K_PASS, :].rearrange("(p j) t -> p j t", j=PACK)
-            for j in range(PACK):
-                raw[a, j] = keep.tile([P, T], F32, name=f"raw{a}_{j}", tag=f"raw{a}_{j}", align_bytes=64)
-                nc.sync.dma_start(out=raw[a, j][:], in_=rows[:, j, :])
+            rows = xT[a * K_PASS : (a + 1) * K_PASS, :].rearrange("(p j) t -> p (j t)", j=PACK)
+            for j in range(0, PACK, 2):
+                pair = keep.tile([P, 2 * T], F32, name=f"pair{a}_{j}", tag=f"pair{a}_{j}", align_bytes=64)
+                nc.sync.dma_start(out=pair[:], in_=rows[:, j * T : (j + 2) * T])
+                raw[a, j], raw[a, j + 1] = pair[:, 0:T], pair[:, T:]
                 if (a, j) == (0, 0):
                     nc.sync.dma_start(out=bias_rows[0:N_TILES, :], in_=b.rearrange("(n p) e -> n (p e)", p=P))
                     nc.sync.dma_start(out=gate_rows[0:N_TILES, :], in_=gate[0, :].rearrange("(n p) -> n p", p=P))
@@ -126,10 +128,10 @@ def tile_moe_res_lin_relu_kernel(tc, xT, xr, w_words, w_scales, b, gate, offs, o
             return offsets[:, c.start // 16 : c.stop // 16]
 
         def gather_on_vector(dst, a, j, c):
-            nc.vector.tensor_copy(dst, raw[a, j][:].indirect(lists(c)))
+            nc.vector.tensor_copy(dst, raw[a, j].indirect(lists(c)))
 
         def gather_on_scalar(dst, a, j, c):
-            nc.scalar.activation(out=dst, in_=raw[a, j][:].indirect(lists(c)), func=COPY)
+            nc.scalar.activation(out=dst, in_=raw[a, j].indirect(lists(c)), func=COPY)
 
         grouped, slot_words, slot_planes = {}, {}, {}
         last = PASSES - 1
@@ -140,7 +142,8 @@ def tile_moe_res_lin_relu_kernel(tc, xT, xr, w_words, w_scales, b, gate, offs, o
             if a == 0:
                 picked[a, 0] = picked[1, 1][:, C:]
             elif a == last:
-                picked[a, 0] = shared.tile([P, PACK * C], F32, name="last_picked", align_bytes=64, offset=0)[:]
+                long_tile = keep.tile([P, (PACK + 2) * C], F32, name="last_picked", align_bytes=64)
+                picked[a, 0] = long_tile[:, 0 : PACK * C]
             else:
                 picked[a, 0] = keep.tile([P, PACK * C], F32, name=f"picked{a}_0", tag=f"picked{a}_0", align_bytes=64)[:]
         for a in range(PASSES):
@@ -163,30 +166,27 @@ def tile_moe_res_lin_relu_kernel(tc, xT, xr, w_words, w_scales, b, gate, offs, o
         for a in range(PASSES):
             for j in range(PACK):
                 row = [picked[a, e][:, j * C : (j + 1) * C] for e in range(E)]
-                if (a, j) == (last, PACK - 1):
-                    gather_on_scalar(row[0][:, 0 : C // 2], a, j, slice(0, C // 2))
-                    gather_on_vector(row[0][:, C // 2 :], a, j, slice(C // 2, C))
-                    gather_on_scalar(row[1], a, j, slots(1))
-                else:
-                    gather_on_scalar(row[0], a, j, slots(0))
-                    gather = gather_on_scalar if j == 0 and a > 0 else gather_on_vector
-                    gather(row[1], a, j, slots(1))
+                for e in range(E):
+                    gather = gather_on_vector if (j, e) in ON_VECTOR[a] else gather_on_scalar
+                    gather(row[e], a, j, slots(e))
             if a + 2 < PASSES:
                 grouped[a, 0] = picked[a + 2, 1][:, HELD : HELD + 2 * C].bitcast(BF16)
+            elif a < last:
+                grouped[a, 0] = long_tile[:, PACK * C - C // 2 : (PACK + 2) * C - C // 2].bitcast(BF16)
             else:
-                grouped[a, 0] = keep.tile([P, C * PACK], BF16, name=f"grouped{a}_0", align_bytes=64)[:]
+                grouped[a, 0] = shared.tile([P, C * PACK], BF16, name="last_grouped0", align_bytes=64, offset=0)[:]
             interleave(a, 0, nc.vector.tensor_copy)
             if 0 < a < last:
-                quantise(a - 1, 1, f"raw{a}_3")
+                quantise(a - 1, 1, f"pair{a}_2")
             quantise(a, 0, f"words{a}")
             if a < last:
-                grouped[a, 1] = grouped[a, 0]
+                grouped[a, 1] = grouped[a, 0] if a + 2 < PASSES else long_tile[:, PACK * C :].bitcast(BF16)
                 nc.gpsimd.tensor_copy(
                     out=grouped[a, 1].rearrange("p (t j) -> p t j", j=PACK),
                     in_=picked[a, 1].rearrange("p (j t) -> p t j", j=PACK),
                 )
             else:
-                grouped[a, 1] = shared.tile([P, C * PACK], BF16, name="last_grouped1", align_bytes=64, offset=4 * C * PACK)[:]
+                grouped[a, 1] = keep.tile([P, C * PACK], BF16, name="last_grouped1", align_bytes=64)[:]
                 quantise(a - 1, 1, None)
                 gates = shared.tile([P, SLOTS], F32, name="gates", align_bytes=64, offset=4 * C)
                 nc.vector.tensor_copy(out=gates[:], in_=gate_bank[:])

from contextlib import ExitStack

import concourse.mybir as mybir
from concourse.masks import make_identity

K, T, E, C, N = 2048, 768, 2, 256, 512
P = 128
PACK = 4
K_PASS = P * PACK
PASSES = K // K_PASS
N_TILES = N // P
SLOTS = E * C
HALVES = C // P
ROWS = 4

F32 = mybir.dt.float32
BF16 = mybir.dt.bfloat16
I32 = mybir.dt.int32
U32 = mybir.dt.uint32
U16 = mybir.dt.uint16
U8 = mybir.dt.uint8
FP8X4 = mybir.dt.float8_e4m3fn_x4
COPY = mybir.ActivationFunctionType.Copy
RELU = mybir.ActivationFunctionType.Relu
ADD = mybir.AluOpType.add
MULT = mybir.AluOpType.mult
MAX = mybir.AluOpType.max

FLOPS = 2 * K * N * E * C
BYTES = 4 * K * T + 2 * 4 * N * T + E * K * N + E * (K // 32) * N + 4 * N * E + 4 * E * C + 2 * P * SLOTS // 16

ON_VECTOR = (((0, 1), (1, 1), (2, 1), (3, 1)), ((1, 1), (2, 1), (3, 1)), ((1, 1), (2, 1), (3, 1)), ((1, 1), (3, 0)))
HELD = 384
SHARE = 352


def tile_moe_res_lin_relu_kernel(tc, xT, xr, w_words, w_scales, b, gate, offs, out):
    nc = tc.nc

    with ExitStack() as ctx:
        keep = ctx.enter_context(tc.tile_pool(name="keep", bufs=1))
        shared = ctx.enter_context(tc.tile_pool(name="shared", bufs=1))
        psum = ctx.enter_context(tc.psum_pool(name="psum", bufs=1))

        def slots(e):
            return slice(e * C, (e + 1) * C)

        bias_rows = keep.tile([P, E * P], F32, name="bias_rows")
        nc.vector.memset(bias_rows[:], 0.0)
        gate_rows = keep.tile([P, P], F32, name="gate_rows")
        nc.vector.memset(gate_rows[:], 0.0)
        identity = keep.tile([P, P], F32, name="identity")
        make_identity(nc, identity[:])

        weight_planes = []
        for e in range(E):
            plane = keep.tile([P, N], U8, name=f"weight_plane{e}", align_bytes=64)
            nc.vector.memset(plane[:].bitcast(I32), 0)
            weight_planes.append(plane)

        windows = []
        for n in range(N_TILES):
            window = keep.tile([P, T], F32, name=f"window{n}")
            if n == 2:
                nc.scalar.copy(out=window[:], in_=windows[0][:])
            else:
                nc.vector.memset(window[:], 0.0)
            windows.append(window)

        offsets = keep.tile([P, SLOTS // 16], U16, name="offsets")
        nc.sync.dma_start(offsets[:], offs)
        raw = {}
        for a in range(PASSES):
            rows = xT[a * K_PASS : (a + 1) * K_PASS, :].rearrange("(p j) t -> p (j t)", j=PACK)
            for j in range(0, PACK, 2):
                pair = keep.tile([P, 2 * T], F32, name=f"pair{a}_{j}", tag=f"pair{a}_{j}", align_bytes=64)
                nc.sync.dma_start(out=pair[:], in_=rows[:, j * T : (j + 2) * T])
                raw[a, j], raw[a, j + 1] = pair[:, 0:T], pair[:, T:]
                if (a, j) == (0, 0):
                    nc.sync.dma_start(out=bias_rows[0:N_TILES, :], in_=b.rearrange("(n p) e -> n (p e)", p=P))
                    nc.sync.dma_start(out=gate_rows[0:N_TILES, :], in_=gate[0, :].rearrange("(n p) -> n p", p=P))

        weights = {}

        def load_weights(e, tiles, passes=range(PASSES)):
            width = len(tiles) * P * PACK
            words = w_words[e].rearrange("a p n r -> p a (n r)")[:, passes.start : passes.stop, tiles[0] * P * PACK : tiles[0] * P * PACK + width]
            name = f"weights{e}_{tiles[0]}_{passes.start}"
            tile = keep.tile([P, len(passes), width], U8, name=name, tag=name, align_bytes=64)
            nc.sync.dma_start(out=tile[:].bitcast(I32), in_=words.bitcast(I32))
            for i, n in enumerate(tiles):
                for a in passes:
                    weights[e, n, a] = tile[:, a - passes.start, i * P * PACK : (i + 1) * P * PACK]

        def load_scales(e):
            for quadrant in range(4):
                nc.sync.dma_start(
                    out=weight_planes[e][32 * quadrant : 32 * quadrant + ROWS * PASSES, :].bitcast(I32),
                    in_=w_scales[e, :, ROWS * quadrant : ROWS * (quadrant + 1), :].bitcast(I32),
                )

        load_scales(0)
        for passes in (range(0, 1), range(1, 2), range(2, PASSES)):
            load_weights(0, (0, 1), passes)
        load_scales(1)
        load_weights(1, (0, 1))
        load_weights(0, (2,))
        load_weights(0, (3,))
        load_weights(1, (2, 3))
        residuals = {}
        for n in range(N_TILES):
            residuals[n] = keep.tile([P, T], F32, name=f"residual{n}", tag=f"residual{n}")
            nc.sync.dma_start(out=residuals[n][:], in_=xr[n * P : (n + 1) * P, :])

        column_bank = psum.tile([P, E + 1, P], F32, name="column_bank", tag="bank0")
        for e in range(E):
            nc.tensor.transpose(column_bank[:, e, :], bias_rows[:, e : E * P : E], identity[:])
        nc.tensor.transpose(column_bank[:, E, :], gate_rows[:], identity[:])
        columns = keep.tile([P, E + 1, N_TILES], F32, name="columns")
        nc.vector.tensor_copy(out=columns[:], in_=column_bank[:, :, 0:N_TILES])
        gate_columns = columns[:, E, :]
        biases = {(n, e): columns[:, e, n : n + 1] for n in range(N_TILES) for e in range(E)}
        gate_bank = psum.tile([P, SLOTS], F32, name="gate_bank", tag="bank1")
        for i in range(E * HALVES):
            nc.tensor.transpose(gate_bank[:, i * P : (i + 1) * P], gate_columns[:, i : i + 1].to_broadcast([P, P]), identity[:])

        def lists(c):
            return offsets[:, c.start // 16 : c.stop // 16]

        def gather_on_vector(dst, a, j, c):
            nc.vector.tensor_copy(dst, raw[a, j].indirect(lists(c)))

        def gather_on_scalar(dst, a, j, c):
            nc.scalar.activation(out=dst, in_=raw[a, j].indirect(lists(c)), func=COPY)

        grouped, slot_words, slot_planes = {}, {}, {}
        last = PASSES - 1
        picked = {}
        for a in range(PASSES):
            picked[a, 1] = keep.tile([P, (PACK + 1) * C], F32, name=f"picked{a}_1", align_bytes=64)[:]
        for a in range(PASSES):
            if a == 0:
                picked[a, 0] = picked[1, 1][:, C:]
            elif a == last:
                long_tile = keep.tile([P, (PACK + 2) * C], F32, name="last_picked", align_bytes=64)
                picked[a, 0] = long_tile[:, 0 : PACK * C]
            else:
                picked[a, 0] = keep.tile([P, PACK * C], F32, name=f"picked{a}_0", tag=f"picked{a}_0", align_bytes=64)[:]
        for a in range(PASSES):
            picked[a, 1] = picked[a, 1][:, 0 : PACK * C]

        def interleave(a, e, copy):
            copy(
                out=grouped[a, e].rearrange("p (c i j) -> p c j i", i=2, j=PACK),
                in_=picked[a, e].rearrange("p (j c i) -> p c j i", i=2, j=PACK),
            )

        def quantise(a, e, tag):
            if tag is None:
                slot_words[a, e] = shared.tile([P, C], U32, name="late_words", align_bytes=64, offset=0)
            else:
                slot_words[a, e] = keep.tile([P, C], U32, name=f"slot_words{a}_{e}", tag=tag, align_bytes=64)
            slot_planes[a, e] = keep.tile([P, C], U8, name=f"slot_plane{a}_{e}", align_bytes=64)
            nc.vector.quantize_mx(out=slot_words[a, e][:].bitcast(FP8X4), scales=slot_planes[a, e][:], in_=grouped[a, e])

        for a in range(PASSES):
            for j in range(PACK):
                row = [picked[a, e][:, j * C : (j + 1) * C] for e in range(E)]
                for e in range(E):
                    gather = gather_on_vector if (j, e) in ON_VECTOR[a] else gather_on_scalar
                    gather(row[e], a, j, slots(e))
            if a + 2 < PASSES:
                grouped[a, 0] = picked[a + 2, 1][:, HELD : HELD + 2 * C].bitcast(BF16)
            elif a < last:
                grouped[a, 0] = long_tile[:, PACK * C - C // 2 : (PACK + 2) * C - C // 2].bitcast(BF16)
            else:
                grouped[a, 0] = shared.tile([P, C * PACK], BF16, name="last_grouped0", align_bytes=64, offset=0)[:]
            interleave(a, 0, nc.vector.tensor_copy)
            if 0 < a < last:
                quantise(a - 1, 1, f"pair{a}_2")
            quantise(a, 0, f"words{a}")
            if a < last:
                grouped[a, 1] = grouped[a, 0] if a + 2 < PASSES else long_tile[:, PACK * C :].bitcast(BF16)
                nc.gpsimd.tensor_copy(
                    out=grouped[a, 1].rearrange("p (t j) -> p t j", j=PACK),
                    in_=picked[a, 1].rearrange("p (j t) -> p t j", j=PACK),
                )
            else:
                grouped[a, 1] = keep.tile([P, C * PACK], BF16, name="last_grouped1", align_bytes=64)[:]
                quantise(a - 1, 1, None)
                gates = shared.tile([P, SLOTS], F32, name="gates", align_bytes=64, offset=4 * C)
                nc.vector.tensor_copy(out=gates[:], in_=gate_bank[:])
                interleave(a, 1, nc.scalar.copy)
                quantise(a, 1, "last_words")

        sums, relu, products = {}, {}, {}

        def open_bank(bank, *units):
            tile = psum.tile([P, len(units) * C], F32, name=f"sums{units[0][0]}_{units[0][1]}", tag=f"bank{bank}")
            for i, unit in enumerate(units):
                sums[unit] = tile[:, i * C : (i + 1) * C]

        def matmuls(n, e, passes=range(PASSES), opens=True, closes=True):
            for a in passes:
                nc.tensor.matmul_mx(
                    out=sums[n, e],
                    lhsT=weights[e, n, a].bitcast(FP8X4),
                    lhsT_scale=weight_planes[e][ROWS * a : P, n * P : (n + 1) * P],
                    rhs=slot_words[a, e][:].bitcast(FP8X4),
                    rhs_scale=slot_planes[a, e][:],
                    start=(opens and a == 0),
                    stop=(closes and a == last),
                )

        def room(tag, width=C):
            return keep.tile([P, width], F32, name=f"on_{tag}", tag=tag)[:]

        def relu_on_scalar(n, e, dst):
            relu[n, e] = dst
            nc.scalar.activation(out=dst, in_=sums[n, e], func=RELU, bias=biases[n, e])

        def relu_on_vector(n, e, dst):
            relu[n, e] = dst
            nc.vector.tensor_scalar(dst, sums[n, e], biases[n, e], 0.0, ADD, MAX)

        def product(n, e, dst):
            products[n, e] = dst
            nc.vector.tensor_tensor(dst, relu[n, e], gate_bank[:, slots(e)], MULT)

        def own(e, c):
            return slice(c.start - e * C, c.stop - e * C)

        def scatter_on_scalar(n, e, c):
            nc.scalar.activation(out=windows[n][:].indirect(lists(c)), in_=products[n, e][:, own(e, c)], func=COPY)

        def scatter_on_vector(n, e, c):
            nc.vector.tensor_copy(windows[n][:].indirect(lists(c)), products[n, e][:, own(e, c)])

        def scatter_product(n, e):
            nc.vector.tensor_tensor(windows[n][:].indirect(lists(slots(e))), relu[n, e], gates[:, slots(e)], MULT)

        def finish(n, lo, hi, engine, result):
            engine.tensor_tensor(result[:, lo:hi], windows[n][:, lo:hi], residuals[n][:, lo:hi], ADD)
            nc.sync.dma_start(out=out[n * P : (n + 1) * P, lo:hi], in_=result[:, lo:hi])

        ring = room("ring", 2 * C)
        low, middle, high = ring[:, 0:C], ring[:, C // 2 : C // 2 + C], ring[:, C:]
        open_bank(0, (0, 0), (1, 0))
        for a in range(PASSES):
            matmuls(0, 0, (a,), closes=False)
            matmuls(1, 0, (a,), opens=False)
        relu_on_scalar(0, 0, middle)
        relu_on_scalar(1, 0, room("relu10"))
        open_bank(0, (2, 0))
        open_bank(2, (0, 1), (1, 1))
        matmuls(2, 0)
        matmuls(0, 1)
        matmuls(1, 1)
        product(0, 0, room("product00"))
        scatter_on_scalar(0, 0, slots(0))
        scatter_product(1, 0)
        relu_on_vector(2, 0, room("relu20"))
        relu_on_scalar(0, 1, low)
        relu_on_scalar(1, 1, high)
        open_bank(0, (3, 0))
        open_bank(2, (2, 1), (3, 1))
        matmuls(3, 0)
        matmuls(2, 1)
        matmuls(3, 1)
        late = keep.tile([P, 2 * C], F32, name="late", tag="weights1_2_0", align_bytes=64)
        product(0, 1, room("product01"))
        scatter_on_scalar(0, 1, slots(1))
        scatter_product(1, 1)
        product(2, 0, late[:, 0:C])
        relu_on_scalar(3, 0, low)
        scatter_on_scalar(2, 0, slots(0))
        relu_on_vector(2, 1, room("relu21"))
        product(3, 0, late[:, C:])
        product(2, 1, room("product21"))
        scatter_on_vector(3, 0, slots(0))
        relu_on_scalar(3, 1, room("relu20"))
        scatter_on_scalar(2, 1, slots(1))
        product(3, 1, low)
        scatter_on_vector(3, 1, slice(C, SHARE))
        scatter_on_scalar(3, 1, slice(SHARE, SLOTS))
        for n in (0, 1):
            finish(n, 0, T, nc.gpsimd, room(f"result{n}", T))
        for n in (2, 3):
            result = room(("relu20", "result3")[n - 2], T)
            for lo in (0, T // 2):
                finish(n, lo, lo + T // 2, nc.vector, result)
